import numpy as np
import ml_dtypes


def mxq(x, axis, fmt="e4m3"):
    dtype, down = {"e4m3": (ml_dtypes.float8_e4m3fn, 7), "e5m2": (ml_dtypes.float8_e5m2, 14)}[fmt]
    v = np.moveaxis(np.asarray(x, np.float32).astype(ml_dtypes.bfloat16).astype(np.float64), axis, -1)
    blocks = v.reshape(v.shape[:-1] + (-1, 32))
    amax = np.abs(blocks).max(-1, keepdims=True)
    byte = np.maximum(np.where(amax > 0, np.frexp(amax)[1] - 1 + 127, 0) - down, 1)
    scale = np.exp2(byte - 127.0)
    codes = (blocks / scale).astype(np.float32).astype(dtype).astype(np.float64)
    return np.moveaxis((codes * scale).reshape(v.shape), -1, axis)


WIDE = False


def mx_kscale(k):
    if not WIDE:
        return np.ones(k)
    levels = np.array([10, -10, 5, -5, 0])
    if k % 512:
        return np.exp2(np.random.permutation(np.resize(levels, k // 32))).repeat(32)
    a = np.empty((k // 512, 16))
    for p in range(k // 512):
        a[p, :8] = np.random.permutation(np.resize(levels, 8))
        for g in range(8):
            far = levels[np.abs(levels - a[p, g]) >= 10]
            a[p, g + 8] = far[np.random.randint(len(far))]
    return np.exp2(a.ravel()).repeat(32)


def f64(x):
    return np.asarray(x).astype(np.float64)


def striped(idx):
    return np.tile(idx.reshape(-1, 16).T, (8, 1)).astype(np.uint16)


def unstriped(offs):
    return offs[:16].T.reshape(-1).astype(np.int64)


E2M1 = np.array([0.0, 0.5, 1.0, 1.5, 2.0, 3.0, 4.0, 6.0, -0.0, -0.5, -1.0, -1.5, -2.0, -3.0, -4.0, -6.0])


def pack_weight(w, fmt):
    k, n = w.shape
    w = f64(np.asarray(w, np.float32).astype(ml_dtypes.bfloat16)).reshape(k // 32, 32, n)
    amax = np.abs(w).max(1)
    if fmt == "e4m3":
        byte = np.frexp(amax)[1] - 1 + 127 - 7
    else:
        mant, ex = np.frexp(amax / 6.0)
        byte = np.where(mant > 0.5, ex, ex - 1) + 127
    byte = np.clip(np.where(amax > 0, byte, 1), 1, 254)
    scaled = (w * np.exp2(127.0 - byte)[:, None, :]).reshape(k, n).astype(np.float32)
    by_word = np.ascontiguousarray(scaled.reshape(k // 512, 128, 4, n).transpose(0, 1, 3, 2))
    if fmt == "e4m3":
        words = by_word.astype(ml_dtypes.float8_e4m3fn).view(np.uint8)
    else:
        c = by_word.astype(ml_dtypes.float4_e2m1fn).view(np.uint8) & 0xF
        words = (c[..., 0::2] | (c[..., 1::2] << 4)).reshape(k // 512, 128, 2 * n)
    return np.ascontiguousarray(words), np.ascontiguousarray(byte.astype(np.uint8).reshape(k // 512, 16, n))


def unpack_weight(words, scales, fmt):
    g, _, n = scales.shape
    words = np.ascontiguousarray(words).reshape(g, 128, n, -1)
    if fmt == "e4m3":
        vals = words.view(ml_dtypes.float8_e4m3fn).astype(np.float64)
    else:
        nib = np.empty((g, 128, n, 4), np.uint8)
        nib[..., 0::2] = words & 0xF
        nib[..., 1::2] = words >> 4
        vals = E2M1[nib]
    vals = vals * np.repeat(np.exp2(scales.astype(np.float64) - 127.0), 8, axis=1)[..., None]
    return vals.transpose(0, 1, 3, 2).reshape(g * 512, n)


def gelu(v):
    return 0.5 * v * (1.0 + np.tanh(np.sqrt(2.0 / np.pi) * (v + 0.044715 * v**3)))


K, K2, T, S, T2, P, H = 1024, 512, 2048, 512, 2048, 1024, 1024

def setup_inputs():
    n = np.random.standard_normal
    s = mx_kscale(K)[:, None]
    s2 = mx_kscale(K2)[:, None]
    u = mx_kscale(H)[:, None]
    d = {}
    d["tab_words"], d["tab_scales"] = pack_weight(n((K, T)) * s, "e4m3")
    d["tab2_words"], d["tab2_scales"] = pack_weight(n((K2, T)) * s2, "e4m3")
    d["offs"] = striped(np.random.permutation(T)[:S])
    d["offs2"] = striped(np.random.permutation(T)[:S])
    perm = np.random.permutation(T2)
    d["offs3"] = striped(perm[:S])
    d["offs4"] = striped(perm[S:2 * S])
    d["offs5"] = striped(np.random.permutation(T2)[:P])
    d["w_tap"] = (0.55 * n((K, H)) / K**0.5 / s).astype(np.float32)
    d["gain"] = (4.0 * np.exp(0.2 * n(H)) * u[:, 0]).astype(np.float32)
    d["w_line"] = (1.2 * n((K2, H)) / K2**0.5 / s2 * u.T).astype(np.float32)
    d["w_tint_words"], d["w_tint_scales"] = pack_weight(1.2 * n((K2, H)) / K2**0.5 / s2 * u.T, "e2m1")
    d["page0"] = (n((H, T2)) * u).astype(np.float32)
    d["wg1"] = np.exp(0.3 * n((128, S))).astype(np.float32)
    d["wg2"] = np.exp(0.3 * n((128, S))).astype(np.float32)
    d["rest"] = (0.8 * n(H) * u[:, 0]).astype(np.float32)
    d["w_read_words"], d["w_read_scales"] = pack_weight(n((H, H)) / H**0.5 / u, "e4m3")
    d["lift"] = (0.8 * np.exp(0.3 * n(H)) / u[:, 0]).astype(np.float32)
    return d

def reference(tab_words, tab_scales, tab2_words, tab2_scales, offs, offs2, offs3, offs4, offs5, w_tap, gain, w_line, w_tint_words, w_tint_scales, page0, wg1, wg2, rest, w_read_words, w_read_scales, lift):
    v = unpack_weight(tab_words, tab_scales, "e4m3")[:, unstriped(offs)]
    v2 = unpack_weight(tab2_words, tab2_scales, "e4m3")[:, unstriped(offs2)]
    h1 = np.sin(mxq(f64(w_tap), 0, "e4m3").T @ v) * f64(gain)[:, None]
    line = mxq(f64(w_line), 0, "e4m3").T @ v2
    tint = unpack_weight(w_tint_words, w_tint_scales, "e2m1").T @ v2
    h2 = np.minimum(line, tint)
    page = f64(page0).copy()
    page[:, unstriped(offs3)] = np.tile(f64(wg1), (H // 128, 1)) * h1
    page[:, unstriped(offs4)] = np.tile(f64(wg2), (H // 128, 1)) * h2
    x = page[:, unstriped(offs5)]
    xq = mxq(x + f64(rest)[:, None], 0, "e4m3")
    y = unpack_weight(w_read_words, w_read_scales, "e4m3").T @ xq
    return y + np.abs(x) * f64(lift)[:, None]

@@ -1,0 +1,355 @@
+import math
+from contextlib import ExitStack
+
+import concourse.mybir as mybir
+from concourse.masks import make_identity
+
+F32 = mybir.dt.float32
+BF16 = mybir.dt.bfloat16
+I32 = mybir.dt.int32
+U32 = mybir.dt.uint32
+U16 = mybir.dt.uint16
+U8 = mybir.dt.uint8
+FP8X4 = mybir.dt.float8_e4m3fn_x4
+FP4X4 = mybir.dt.float4_e2m1fn_x4
+ACT = mybir.ActivationFunctionType
+ALU = mybir.AluOpType
+
+P = 128
+PACK = 4
+BLK = P * PACK
+SLOTS = 2048
+S = 512
+H = 1024
+NB = H // BLK
+QUADS = 4
+ROUNDER = 12582912.0
+
+FLOPS = 4294967296
+
+
+def tile_list_slate_cleavage_board_kernel(
+    tc, tab_words, tab_scales, tab2_words, tab2_scales, offs, offs2, offs3, offs4, offs5,
+    w_tap, gain, w_line, w_tint_words, w_tint_scales, page0, wg1, wg2, rest,
+    w_read_words, w_read_scales, lift, out,
+):
+    nc = tc.nc
+    with ExitStack() as ctx:
+        lists = ctx.enter_context(tc.tile_pool(name="lists", bufs=1))
+        keep = ctx.enter_context(tc.tile_pool(name="keep", bufs=1))
+        ring = ctx.enter_context(tc.tile_pool(name="ring", bufs=2))
+        psum = ctx.enter_context(tc.psum_pool(name="psum", bufs=8))
+
+        def load_list(src, name):
+            tile = lists.tile(list(src.shape), U16, name=name)
+            nc.sync.dma_start(tile[:], src)
+            return tile
+
+        def slot(tag, shape, dtype, name):
+            return keep.tile(shape, dtype, name=name, tag=tag, align_bytes=64)
+
+        def zeroed_plane(engine, width, name):
+            plane = keep.tile([P, width], U8, name=name, align_bytes=64)
+            engine.memset(plane[:].bitcast(I32), 0)
+            return plane
+
+        def load_scale_rows(queue, plane, scales):
+            rows = 4 * scales.shape[0]
+            for q in range(QUADS):
+                queue.dma_start(
+                    plane[32 * q : 32 * q + rows, :].bitcast(I32),
+                    scales[:, 4 * q : 4 * q + 4, :].bitcast(I32),
+                )
+
+        def load_words(tag, words, name):
+            tile = slot(tag, [P, SLOTS], U32, name)
+            nc.sync.dma_start(tile[:].bitcast(I32), words.rearrange("p t i -> p (t i)").bitcast(I32))
+            return tile
+
+        def load_weight(tag, w, a, b, name):
+            raw = slot(tag, [P, PACK, BLK], F32, name)
+            rows = w[a * BLK : (a + 1) * BLK, b * BLK : (b + 1) * BLK]
+            nc.sync.dma_start(raw[:], rows.rearrange("(p j) c -> p j c", j=PACK))
+            return raw
+
+        def load_page(b, t):
+            name = "page%d%d" % (b, t)
+            page = slot("s1" if (b, t) == (1, 3) else name, [P, SLOTS], F32, name)
+            nc.sync.dma_start(page[:], page0.rearrange("(b p t) s -> b t p s", b=NB, t=PACK)[b, t])
+            return page
+
+        def load_dealt(tag, wg, name):
+            tile = slot(tag, [P, PACK, S], F32, name)
+            for q in range(QUADS):
+                nc.sync.dma_start(tile[32 * q : 32 * q + 32, :, :], wg.rearrange("(m t) j -> m t j", t=PACK))
+            return tile
+
+        def gather(dtype, window, offsets, name):
+            picked = keep.tile([P, S], dtype, name=name, align_bytes=64)
+            nc.vector.tensor_copy(picked[:], window[:].indirect(offsets[:]))
+            return picked
+
+        def round_weight(copy, raw):
+            grouped = ring.tile([P, BLK * PACK], BF16, name="grouped", tag="grouped", bufs=3, align_bytes=64)
+            copy(
+                grouped[:].rearrange("p (t m j) -> p m t j", t=PACK, j=PACK),
+                raw[:].rearrange("p j (m t) -> p m t j", t=PACK),
+            )
+            return grouped
+
+        def quantise(grouped, name):
+            codes = keep.tile([P, BLK], U32, name=name + "_codes", align_bytes=64)
+            plane = keep.tile([P, BLK], U8, name=name + "_plane", align_bytes=64)
+            nc.vector.quantize_mx(out=codes[:].bitcast(FP8X4), scales=plane[:], in_=grouped[:])
+            return codes, plane
+
+        def deal_plane(plane, name):
+            dealt = keep.tile([P, H], U8, name=name, align_bytes=64)
+            nc.vector.tensor_copy(
+                dealt[:].rearrange("p (b t mo mi) -> p b mo t mi", b=NB, t=PACK, mi=16),
+                plane[:].rearrange("p (b mo mi t) -> p b mo t mi", b=NB, t=PACK, mi=16),
+            )
+            return dealt
+
+        def bank():
+            return psum.tile([P, S], F32, name="bank", tag="bank")
+
+        def cols(t):
+            return slice(t * P, (t + 1) * P)
+
+        tiles = [(b, t) for b in range(NB) for t in range(PACK)]
+
+        tint_plane_raw = zeroed_plane(nc.vector, H, "tint_plane_raw")
+        v_plane_all = zeroed_plane(nc.vector, SLOTS, "v_plane_all")
+        read_plane_raw = zeroed_plane(nc.vector, H, "read_plane_raw")
+
+        idx2 = load_list(offs2, "idx2")
+        v2_plane_all = keep.tile([P, SLOTS], U8, name="v2_plane_all", align_bytes=64)
+        for q in range(QUADS):
+            rows = tab2_scales[0, 4 * q : 4 * q + 4, :].bitcast(I32)
+            nc.sync.dma_start(
+                v2_plane_all[32 * q : 32 * q + 32, :].bitcast(I32),
+                rows.unsqueeze(0).broadcast_to([8, 4, SLOTS // 4]),
+            )
+        v2_all = load_words("s0", tab2_words[0], "v2_all")
+        tint_raw = keep.tile([P, 2 * H], U8, name="tint_raw", align_bytes=64)
+        nc.sync.dma_start(tint_raw[:].bitcast(I32), w_tint_words[0].bitcast(I32))
+        line_raw = {0: load_weight("s1", w_line, 0, 0, "line_raw0")}
+        load_scale_rows(nc.scalar, tint_plane_raw, w_tint_scales)
+        idx4 = load_list(offs4, "idx4")
+        wg2_sb = load_dealt("wg2", wg2, "wg2_sb")
+        pages = {(0, 0): load_page(0, 0)}
+        ident = keep.tile([P, P], F32, name="ident")
+        make_identity(nc, ident[:])
+        vec_rows = keep.tile([P, BLK], F32, name="vec_rows")
+        nc.gpsimd.memset(vec_rows[:], 0.0)
+
+        tint_words = keep.tile([P, 2 * H], U8, name="tint_words", align_bytes=64)
+        for b in range(NB):
+            half = slice(b * 2 * BLK, (b + 1) * 2 * BLK)
+            nc.vector.tensor_copy(
+                tint_words[:, half].rearrange("p (t mo mi e) -> p mo t mi e", t=PACK, mi=8, e=2),
+                tint_raw[:, half].rearrange("p (mo mi t e) -> p mo t mi e", t=PACK, mi=8, e=2),
+            )
+        tint_plane = deal_plane(tint_plane_raw, "tint_plane")
+        v2_words = gather(U32, v2_all, idx2, "v2_words")
+        v2_plane = gather(U8, v2_plane_all, idx2, "v2_plane")
+        line_q = {0: quantise(round_weight(nc.vector.tensor_copy, line_raw[0]), "line0")}
+
+        def put_h2(b, t):
+            c = b * PACK + t
+            tint_ps = bank()
+            nc.tensor.matmul_mx(
+                out=tint_ps[:],
+                lhsT=tint_words[:, 2 * c * P : 2 * (c + 1) * P].bitcast(FP4X4), lhsT_scale=tint_plane[:, cols(c)],
+                rhs=v2_words[:].bitcast(FP8X4), rhs_scale=v2_plane[:], start=True, stop=True,
+            )
+            line_ps = bank()
+            codes, plane = line_q[b]
+            nc.tensor.matmul_mx(
+                out=line_ps[:],
+                lhsT=codes[:, cols(t)].bitcast(FP8X4), lhsT_scale=plane[:, cols(t)],
+                rhs=v2_words[:].bitcast(FP8X4), rhs_scale=v2_plane[:], start=True, stop=True,
+            )
+            tint_sb = ring.tile([P, S], F32, name="tint_sb")
+            nc.scalar.copy(tint_sb[:], tint_ps[:])
+            h2 = ring.tile([P, S], F32, name="h2")
+            nc.vector.tensor_tensor(h2[:], line_ps[:], tint_sb[:], ALU.min)
+            nc.vector.tensor_tensor(pages[b, t][:].indirect(idx4[:]), h2[:], wg2_sb[:, t, :], ALU.mult)
+
+        pages[0, 1] = load_page(0, 1)
+        line_raw[1] = load_weight("s2", w_line, 0, 1, "line_raw1")
+        pages[0, 2] = load_page(0, 2)
+        pages[0, 3] = load_page(0, 3)
+        idx = load_list(offs, "idx")
+        idx3 = load_list(offs3, "idx3")
+        idx5 = load_list(offs5, "idx5")
+        load_scale_rows(nc.sync, v_plane_all, tab_scales)
+        v_all = [load_words("s3", tab_words[0], "v_all0"), load_words("s4", tab_words[1], "v_all1")]
+        pages[1, 0] = load_page(1, 0)
+
+        put_h2(0, 0)
+        put_h2(0, 1)
+        line_q[1] = quantise(round_weight(nc.scalar.copy, line_raw[1]), "line1")
+        put_h2(0, 2)
+        put_h2(0, 3)
+
+        tap_raw = {(0, 0): load_weight("s5", w_tap, 0, 0, "tap_raw00"), (1, 0): load_weight("s6", w_tap, 1, 0, "tap_raw10")}
+        pages[1, 1] = load_page(1, 1)
+
+        v_words = [gather(U32, v_all[a], idx, "v_words%d" % a) for a in range(2)]
+        v_plane = gather(U8, v_plane_all, idx, "v_plane")
+
+        tap_raw[0, 1] = load_weight("s7", w_tap, 0, 1, "tap_raw01")
+        pages[1, 2] = load_page(1, 2)
+        tap_raw[1, 1] = load_weight("s8", w_tap, 1, 1, "tap_raw11")
+
+        put_h2(1, 0)
+        tap_q = {}
+        for a in range(2):
+            tap_q[a, 0] = quantise(round_weight(nc.scalar.copy, tap_raw[a, 0]), "tap%d0" % a)
+        load_scale_rows(nc.sync, read_plane_raw, w_read_scales)
+        read_raw = slot("s0", [P, 2 * H], I32, "read_raw")
+        nc.sync.dma_start(read_raw[:].rearrange("p (a c) -> p a c", a=2), w_read_words.rearrange("a p c i -> p a (c i)").bitcast(I32))
+        pages[1, 3] = load_page(1, 3)
+        for v, vec in enumerate((gain, rest, lift)):
+            nc.sync.dma_start(vec_rows[NB * v : NB * (v + 1), :], vec.rearrange("(b c) -> b c", b=NB))
+        vec_ps = bank()
+        for t in range(PACK):
+            nc.tensor.transpose(vec_ps[:, cols(t)], vec_rows[:, t:BLK:PACK], ident[:])
+        vec_sb = keep.tile([P, PACK, 8], F32, name="vec_sb")
+        nc.scalar.copy(vec_sb[:], vec_ps[:].rearrange("p (t r) -> p t r", t=PACK)[:, :, 0:8])
+
+        def channel(v, b, t):
+            return vec_sb[:, t, NB * v + b : NB * v + b + 1]
+
+        wg1_sb = load_dealt("s2", wg1, "wg1_sb")
+        put_h2(1, 1)
+
+        gated = {0: slot("s5", [P, PACK, S], F32, "gated0"), 1: wg1_sb}
+        sines = {}
+
+        turns = {}
+
+        def tap_product(b, t):
+            prod = bank()
+            for jb in range(PACK):
+                for a in range(2):
+                    codes, plane = tap_q[a, b]
+                    nc.tensor.matmul_mx(
+                        out=prod[:, cols(jb)],
+                        lhsT=v_words[a][:, cols(jb)].bitcast(FP8X4), lhsT_scale=v_plane[4 * a : P, cols(jb)],
+                        rhs=codes[:, cols(t)].bitcast(FP8X4), rhs_scale=plane[:, cols(t)],
+                        start=(a == 0), stop=(a == 1),
+                    )
+            u = ring.tile([P, S], F32, name="u")
+            whole = ring.tile([P, S], U32, name="whole")
+            minus_whole = ring.tile([P, S], F32, name="minus_whole")
+            nc.scalar.activation(whole[:], prod[:], ACT.Copy, scale=0.5 / math.pi, bias=ROUNDER)
+            nc.scalar.activation(u[:], prod[:], ACT.Copy, scale=0.5 / math.pi)
+            nc.scalar.activation(minus_whole[:], whole[:], ACT.Copy, scale=-1.0, bias=ROUNDER)
+            frac = bank()
+            for jb in range(PACK):
+                nc.tensor.matmul(frac[:, cols(jb)], u[:, cols(jb)], ident[:], start=True, stop=False, is_transpose=True)
+                nc.tensor.matmul(frac[:, cols(jb)], minus_whole[:, cols(jb)], ident[:], start=False, stop=True, is_transpose=True)
+            turns[b, t] = frac
+
+        def make_h1(b, t):
+            nc.scalar.activation(gated[b][:, t, :], wg1_sb[:, t, :], ACT.Copy, scale=channel(0, b, t))
+            sines[b, t] = ring.tile([P, S], F32, name="sine", bufs=3)
+            nc.scalar.activation(sines[b, t][:], turns[b, t][:], ACT.Sin, scale=2.0 * math.pi)
+
+        def put_h1(b, t):
+            nc.vector.tensor_tensor(pages[b, t][:].indirect(idx3[:]), sines[b, t][:], gated[b][:, t, :], ALU.mult)
+
+        x_tag = {(0, 0): "s3", (0, 1): "s4", (1, 0): "s5", (1, 1): "s2"}
+        xs, rested, x_q = {}, {}, {}
+
+        def fetch(b, t, h):
+            if t == 0:
+                xs[b, h] = slot(x_tag[b, h], [P, PACK, S], F32, "x%d%d" % (b, h))
+            nc.vector.tensor_copy(xs[b, h][:, t, :], pages[b, t][:].indirect(idx5[:, 32 * h : 32 * (h + 1)]))
+
+        def add_rest(b, t, h):
+            if t == 0:
+                rested[b, h] = ring.tile([P, PACK, S], BF16, name="rested")
+            nc.scalar.activation(rested[b, h][:, t, :], xs[b, h][:, t, :], ACT.Identity, bias=channel(1, b, t))
+
+        def take_abs(b, t, h):
+            nc.scalar.activation(xs[b, h][:, t, :], xs[b, h][:, t, :], ACT.Abs)
+
+        def quantise_x(b, h):
+            grouped = ring.tile([P, S * PACK], BF16, name="grouped", tag="grouped", bufs=3, align_bytes=64)
+            nc.scalar.copy(
+                grouped[:].rearrange("p (c i t) -> p c t i", i=4, t=PACK),
+                rested[b, h][:].rearrange("p t (c i) -> p c t i", i=4),
+            )
+            x_q[b, h] = quantise(grouped, "x%d%d" % (b, h))
+
+        tap_q[0, 1] = quantise(round_weight(nc.scalar.copy, tap_raw[0, 1]), "tap01")
+        put_h2(1, 2)
+        tap_q[1, 1] = quantise(round_weight(nc.scalar.copy, tap_raw[1, 1]), "tap11")
+        put_h2(1, 3)
+        for i in range(3):
+            tap_product(*tiles[i])
+        make_h1(0, 0)
+
+        read_words = slot("s6", [P, 2 * H], I32, "read_words")
+        nc.vector.tensor_copy(
+            read_words[:].rearrange("p (g t mo mi) -> p g mo t mi", g=2 * NB, t=PACK, mi=4),
+            read_raw[:].rearrange("p (g mo mi t) -> p g mo t mi", g=2 * NB, t=PACK, mi=4),
+        )
+        read_plane = deal_plane(read_plane_raw, "read_plane")
+
+        def after_fetch(i):
+            b, t = tiles[i]
+            for h in range(2 - b):
+                add_rest(b, t, h)
+            for h in range(2 - b):
+                if t == PACK - 1:
+                    quantise_x(b, h)
+                take_abs(b, t, h)
+
+        for i, (b, t) in enumerate(tiles):
+            if i + 1 < len(tiles):
+                make_h1(*tiles[i + 1])
+            put_h1(b, t)
+            for h in range(2 - b):
+                fetch(b, t, h)
+            if i + 3 < len(tiles):
+                tap_product(*tiles[i + 3])
+            if i >= 1:
+                after_fetch(i - 1)
+        for t in range(PACK):
+            fetch(1, t, 1)
+        after_fetch(len(tiles) - 1)
+        for t in range(PACK):
+            add_rest(1, t, 1)
+
+        out_rows = out.rearrange("(b p t) j -> b t p j", b=NB, t=PACK)
+
+        def finish(b, t, h):
+            c = b * PACK + t
+            y = bank()
+            for a in range(2):
+                codes, plane = x_q[a, h]
+                nc.tensor.matmul_mx(
+                    out=y[:],
+                    lhsT=read_words[:, a * H + c * P : a * H + (c + 1) * P].bitcast(FP8X4),
+                    lhsT_scale=read_plane[4 * a : P, cols(c)],
+                    rhs=codes[:].bitcast(FP8X4), rhs_scale=plane[:],
+                    start=(a == 0), stop=(a == 1),
+                )
+            res = xs[b, h][:, t, :]
+            nc.vector.scalar_tensor_tensor(res, res, channel(2, b, t), y[:], ALU.mult, ALU.add)
+            nc.sync.dma_start(out_rows[b, t][:, h * S : (h + 1) * S], res)
+
+        for b, t in tiles[:PACK]:
+            finish(b, t, 0)
+        quantise_x(1, 1)
+        for t in range(PACK):
+            take_abs(1, t, 1)
+        for b, t in tiles[PACK:]:
+            finish(b, t, 0)
+        for b, t in tiles:
+            finish(b, t, 1)

@@ -38,7 +38,7 @@ def tile_list_slate_cleavage_board_kernel(
         lists = ctx.enter_context(tc.tile_pool(name="lists", bufs=1))
         keep = ctx.enter_context(tc.tile_pool(name="keep", bufs=1))
         ring = ctx.enter_context(tc.tile_pool(name="ring", bufs=2))
-        psum = ctx.enter_context(tc.psum_pool(name="psum", bufs=8))
+        psum = ctx.enter_context(tc.psum_pool(name="psum", bufs=2))
 
         def load_list(src, name):
             tile = lists.tile(list(src.shape), U16, name=name)
@@ -78,143 +78,169 @@ def tile_list_slate_cleavage_board_kernel(
             nc.sync.dma_start(page[:], page0.rearrange("(b p t) s -> b t p s", b=NB, t=PACK)[b, t])
             return page
 
-        def load_dealt(tag, wg, name):
-            tile = slot(tag, [P, PACK, S], F32, name)
-            for q in range(QUADS):
-                nc.sync.dma_start(tile[32 * q : 32 * q + 32, :, :], wg.rearrange("(m t) j -> m t j", t=PACK))
+        def load_rows(wg, name, tag):
+            tile = slot(tag, [P, S], F32, name)
+            nc.sync.dma_start(tile[:], wg)
             return tile
 
-        def gather(dtype, window, offsets, name):
-            picked = keep.tile([P, S], dtype, name=name, align_bytes=64)
+        def turn(src, tag):
+            turned = bank(tag)
+            for jb in range(PACK):
+                nc.tensor.transpose(turned[:, cols(jb)], src[:, cols(jb)], ident[:])
+            return turned
+
+        def deal_rows(turned, t):
+            picked = ring.tile([P, S], F32, name="picked")
+            columns = turned[:].rearrange("p (jb m t) -> p jb t m", jb=PACK, t=PACK)[:, :, t, :]
+            nc.scalar.copy(
+                picked[:].rearrange("p (jb q m) -> p jb q m", jb=PACK, q=QUADS),
+                columns.unsqueeze(2).broadcast_to([P, PACK, QUADS, 32]),
+            )
+            return turn(picked, "turned")
+
+        def gather(dtype, window, offsets, name, tag=None):
+            picked = slot(tag or name, [P, S], dtype, name)
             nc.vector.tensor_copy(picked[:], window[:].indirect(offsets[:]))
             return picked
 
-        def round_weight(copy, raw):
-            grouped = ring.tile([P, BLK * PACK], BF16, name="grouped", tag="grouped", bufs=3, align_bytes=64)
+        def round_weight(copy, raw, tag):
+            grouped = slot(tag, [P, BLK * PACK], BF16, "grouped")
             copy(
                 grouped[:].rearrange("p (t m j) -> p m t j", t=PACK, j=PACK),
                 raw[:].rearrange("p j (m t) -> p m t j", t=PACK),
             )
             return grouped
 
-        def quantise(grouped, name):
-            codes = keep.tile([P, BLK], U32, name=name + "_codes", align_bytes=64)
+        def quantise(grouped, name, tag=None):
+            codes = slot(tag or name, [P, BLK], U32, name + "_codes")
             plane = keep.tile([P, BLK], U8, name=name + "_plane", align_bytes=64)
             nc.vector.quantize_mx(out=codes[:].bitcast(FP8X4), scales=plane[:], in_=grouped[:])
             return codes, plane
 
-        def deal_plane(plane, name):
-            dealt = keep.tile([P, H], U8, name=name, align_bytes=64)
+        def deal_plane(plane, name, tag):
+            dealt = slot(tag, [P, H], U8, name)
             nc.vector.tensor_copy(
                 dealt[:].rearrange("p (b t mo mi) -> p b mo t mi", b=NB, t=PACK, mi=16),
                 plane[:].rearrange("p (b mo mi t) -> p b mo t mi", b=NB, t=PACK, mi=16),
             )
             return dealt
 
-        def bank():
-            return psum.tile([P, S], F32, name="bank", tag="bank")
+        def bank(tag):
+            return psum.tile([P, S], F32, name=tag, tag=tag)
 
         def cols(t):
             return slice(t * P, (t + 1) * P)
 
         tiles = [(b, t) for b in range(NB) for t in range(PACK)]
 
-        tint_plane_raw = zeroed_plane(nc.vector, H, "tint_plane_raw")
-        v_plane_all = zeroed_plane(nc.vector, SLOTS, "v_plane_all")
-        read_plane_raw = zeroed_plane(nc.vector, H, "read_plane_raw")
-
-        idx2 = load_list(offs2, "idx2")
-        v2_plane_all = keep.tile([P, SLOTS], U8, name="v2_plane_all", align_bytes=64)
-        for q in range(QUADS):
-            rows = tab2_scales[0, 4 * q : 4 * q + 4, :].bitcast(I32)
-            nc.sync.dma_start(
-                v2_plane_all[32 * q : 32 * q + 32, :].bitcast(I32),
-                rows.unsqueeze(0).broadcast_to([8, 4, SLOTS // 4]),
-            )
-        v2_all = load_words("s0", tab2_words[0], "v2_all")
-        tint_raw = keep.tile([P, 2 * H], U8, name="tint_raw", align_bytes=64)
-        nc.sync.dma_start(tint_raw[:].bitcast(I32), w_tint_words[0].bitcast(I32))
-        line_raw = {0: load_weight("s1", w_line, 0, 0, "line_raw0")}
-        load_scale_rows(nc.scalar, tint_plane_raw, w_tint_scales)
-        idx4 = load_list(offs4, "idx4")
-        wg2_sb = load_dealt("wg2", wg2, "wg2_sb")
-        pages = {(0, 0): load_page(0, 0)}
         ident = keep.tile([P, P], F32, name="ident")
         make_identity(nc, ident[:])
+        v2_plane_all = zeroed_plane(nc.vector, SLOTS, "v2_plane_all")
+        v_plane_all = zeroed_plane(nc.gpsimd, SLOTS, "v_plane_all")
+        read_plane_raw = zeroed_plane(nc.gpsimd, H, "read_plane_raw")
         vec_rows = keep.tile([P, BLK], F32, name="vec_rows")
         nc.gpsimd.memset(vec_rows[:], 0.0)
 
-        tint_words = keep.tile([P, 2 * H], U8, name="tint_words", align_bytes=64)
+        idx2 = load_list(offs2, "idx2")
+        wg2_rows = load_rows(wg2, "wg2_rows", "wg_rows")
+        tint_plane_raw = keep.tile([P, H], U8, name="tint_plane_raw", align_bytes=64)
+        for q in range(QUADS):
+            rows = w_tint_scales[0, 4 * q : 4 * q + 4, :].bitcast(I32)
+            nc.sync.dma_start(
+                tint_plane_raw[32 * q : 32 * q + 32, :].bitcast(I32),
+                rows.unsqueeze(0).broadcast_to([8, 4, H // 4]),
+            )
+        tint_raw = keep.tile([P, 2 * H], U8, name="tint_raw", align_bytes=64)
+        nc.sync.dma_start(tint_raw[:].bitcast(I32), w_tint_words[0].bitcast(I32))
+        line_raw = {0: load_weight("s1", w_line, 0, 0, "line_raw0")}
+        load_scale_rows(nc.sync, v2_plane_all, tab2_scales)
+        v2_all = load_words("s0", tab2_words[0], "v2_all")
+        idx4 = load_list(offs4, "idx4")
+        load_scale_rows(nc.sync, v_plane_all, tab_scales)
+        idx = load_list(offs, "idx")
+        pages = {(0, 0): load_page(0, 0)}
+        wg2_turned = turn(wg2_rows, "tap")
+        for v, vec in enumerate((gain, rest, lift)):
+            nc.sync.dma_start(vec_rows[NB * v : NB * (v + 1), :], vec.rearrange("(b c) -> b c", b=NB))
+        wg1_rows = load_rows(wg1, "wg1_rows", "wg_rows")
+        pages[0, 1] = load_page(0, 1)
+        v_all = [load_words("s3", tab_words[0], "v_all0"), load_words("s4", tab_words[1], "v_all1")]
+        pages[0, 2] = load_page(0, 2)
+        line_raw[1] = load_weight("s2", w_line, 0, 1, "line_raw1")
+        pages[0, 3] = load_page(0, 3)
+        tap_raw = {(a, 0): load_weight("s%d" % (5 + a), w_tap, a, 0, "tap_raw%d0" % a) for a in range(2)}
+        tap_raw[0, 1] = load_weight("s7", w_tap, 0, 1, "tap_raw01")
+        tap_raw[1, 1] = load_weight("s8", w_tap, 1, 1, "tap_raw11")
+        pages[1, 0] = load_page(1, 0)
+        pages[1, 1] = load_page(1, 1)
+        load_scale_rows(nc.sync, read_plane_raw, w_read_scales)
+        pages[1, 2] = load_page(1, 2)
+        idx3 = load_list(offs3, "idx3")
+        idx5 = load_list(offs5, "idx5")
+
+        wg2_dealt = []
+        tint_words = slot("g1", [P, 2 * H], U8, "tint_words")
         for b in range(NB):
             half = slice(b * 2 * BLK, (b + 1) * 2 * BLK)
             nc.vector.tensor_copy(
                 tint_words[:, half].rearrange("p (t mo mi e) -> p mo t mi e", t=PACK, mi=8, e=2),
                 tint_raw[:, half].rearrange("p (mo mi t e) -> p mo t mi e", t=PACK, mi=8, e=2),
             )
-        tint_plane = deal_plane(tint_plane_raw, "tint_plane")
-        v2_words = gather(U32, v2_all, idx2, "v2_words")
+        tint_plane = deal_plane(tint_plane_raw, "tint_plane", "g3")
+        line_grouped = round_weight(nc.vector.tensor_copy, line_raw[0], "g2")
         v2_plane = gather(U8, v2_plane_all, idx2, "v2_plane")
-        line_q = {0: quantise(round_weight(nc.vector.tensor_copy, line_raw[0]), "line0")}
+        line_q = {0: quantise(line_grouped, "line0")}
+        v2_words = gather(U32, v2_all, idx2, "v2_words")
 
-        def put_h2(b, t):
-            c = b * PACK + t
-            tint_ps = bank()
+        read_raw = slot("s0", [P, 2 * H], I32, "read_raw")
+        nc.sync.dma_start(read_raw[:].rearrange("p (a c) -> p a c", a=2), w_read_words.rearrange("a p c i -> p a (c i)").bitcast(I32))
+        pages[1, 3] = load_page(1, 3)
+
+        h2 = []
+
+        def start_h2(c):
+            if c < PACK:
+                wg2_dealt.append(slot("w%d" % c, [P, S], F32, "wg2_dealt%d" % c))
+                nc.scalar.copy(wg2_dealt[c][:], deal_rows(wg2_turned, c)[:])
+            tint_ps = bank("tint")
             nc.tensor.matmul_mx(
                 out=tint_ps[:],
                 lhsT=tint_words[:, 2 * c * P : 2 * (c + 1) * P].bitcast(FP4X4), lhsT_scale=tint_plane[:, cols(c)],
                 rhs=v2_words[:].bitcast(FP8X4), rhs_scale=v2_plane[:], start=True, stop=True,
             )
-            line_ps = bank()
+            h2.append(slot("h%d" % c, [P, S], F32, "h2_%d" % c))
+            nc.scalar.copy(h2[c][:], tint_ps[:])
+
+        def put_h2(c):
+            b, t = tiles[c]
+            line_ps = bank("line")
             codes, plane = line_q[b]
             nc.tensor.matmul_mx(
                 out=line_ps[:],
                 lhsT=codes[:, cols(t)].bitcast(FP8X4), lhsT_scale=plane[:, cols(t)],
                 rhs=v2_words[:].bitcast(FP8X4), rhs_scale=v2_plane[:], start=True, stop=True,
             )
-            tint_sb = ring.tile([P, S], F32, name="tint_sb")
-            nc.scalar.copy(tint_sb[:], tint_ps[:])
-            h2 = ring.tile([P, S], F32, name="h2")
-            nc.vector.tensor_tensor(h2[:], line_ps[:], tint_sb[:], ALU.min)
-            nc.vector.tensor_tensor(pages[b, t][:].indirect(idx4[:]), h2[:], wg2_sb[:, t, :], ALU.mult)
+            nc.vector.tensor_tensor(h2[c][:], line_ps[:], h2[c][:], ALU.min)
+            nc.vector.tensor_tensor(pages[b, t][:].indirect(idx4[:]), h2[c][:], wg2_dealt[t][:], ALU.mult)
 
-        pages[0, 1] = load_page(0, 1)
-        line_raw[1] = load_weight("s2", w_line, 0, 1, "line_raw1")
-        pages[0, 2] = load_page(0, 2)
-        pages[0, 3] = load_page(0, 3)
-        idx = load_list(offs, "idx")
-        idx3 = load_list(offs3, "idx3")
-        idx5 = load_list(offs5, "idx5")
-        load_scale_rows(nc.sync, v_plane_all, tab_scales)
-        v_all = [load_words("s3", tab_words[0], "v_all0"), load_words("s4", tab_words[1], "v_all1")]
-        pages[1, 0] = load_page(1, 0)
-
-        put_h2(0, 0)
-        put_h2(0, 1)
-        line_q[1] = quantise(round_weight(nc.scalar.copy, line_raw[1]), "line1")
-        put_h2(0, 2)
-        put_h2(0, 3)
-
-        tap_raw = {(0, 0): load_weight("s5", w_tap, 0, 0, "tap_raw00"), (1, 0): load_weight("s6", w_tap, 1, 0, "tap_raw10")}
-        pages[1, 1] = load_page(1, 1)
-
-        v_words = [gather(U32, v_all[a], idx, "v_words%d" % a) for a in range(2)]
+        for c in range(2):
+            start_h2(c)
+        put_h2(0)
         v_plane = gather(U8, v_plane_all, idx, "v_plane")
+        put_h2(1)
+        for c in range(2, len(tiles)):
+            start_h2(c)
+        v_words = [gather(U32, v_all[0], idx, "v_words0", "h0")]
+        put_h2(2)
+        put_h2(3)
+        line_q[1] = quantise(round_weight(nc.scalar.copy, line_raw[1], "g1"), "line1", "h3")
+        v_words.append(gather(U32, v_all[1], idx, "v_words1", "g1"))
+        tap_grouped = {
+            (a, b): round_weight(nc.scalar.copy, tap_raw[a, b], (("g3", "g2"), ("h1", "h2"))[b][a])
+            for b in range(NB) for a in range(2)
+        }
 
-        tap_raw[0, 1] = load_weight("s7", w_tap, 0, 1, "tap_raw01")
-        pages[1, 2] = load_page(1, 2)
-        tap_raw[1, 1] = load_weight("s8", w_tap, 1, 1, "tap_raw11")
-
-        put_h2(1, 0)
-        tap_q = {}
-        for a in range(2):
-            tap_q[a, 0] = quantise(round_weight(nc.scalar.copy, tap_raw[a, 0]), "tap%d0" % a)
-        load_scale_rows(nc.sync, read_plane_raw, w_read_scales)
-        read_raw = slot("s0", [P, 2 * H], I32, "read_raw")
-        nc.sync.dma_start(read_raw[:].rearrange("p (a c) -> p a c", a=2), w_read_words.rearrange("a p c i -> p a (c i)").bitcast(I32))
-        pages[1, 3] = load_page(1, 3)
-        for v, vec in enumerate((gain, rest, lift)):
-            nc.sync.dma_start(vec_rows[NB * v : NB * (v + 1), :], vec.rearrange("(b c) -> b c", b=NB))
-        vec_ps = bank()
+        vec_ps = bank("turned")
         for t in range(PACK):
             nc.tensor.transpose(vec_ps[:, cols(t)], vec_rows[:, t:BLK:PACK], ident[:])
         vec_sb = keep.tile([P, PACK, 8], F32, name="vec_sb")
@@ -223,16 +249,22 @@ def tile_list_slate_cleavage_board_kernel(
         def channel(v, b, t):
             return vec_sb[:, t, NB * v + b : NB * v + b + 1]
 
-        wg1_sb = load_dealt("s2", wg1, "wg1_sb")
-        put_h2(1, 1)
+        put_h2(4)
+        tap_q = {(a, 0): quantise(tap_grouped[a, 0], "tap%d0" % a, ("h4", "w0")[a]) for a in range(2)}
+        put_h2(5)
 
-        gated = {0: slot("s5", [P, PACK, S], F32, "gated0"), 1: wg1_sb}
+        gated = [keep.tile([P, PACK, S], F32, name="gated%d" % b) for b in range(NB)]
+        wg1_turned = turn(wg1_rows, "tint")
+        for t in range(PACK):
+            dealt = deal_rows(wg1_turned, t)
+            for b in range(NB):
+                nc.scalar.activation(gated[b][:, t, :], dealt[:], ACT.Copy, scale=channel(0, b, t))
         sines = {}
 
         turns = {}
 
         def tap_product(b, t):
-            prod = bank()
+            prod = bank("tap")
             for jb in range(PACK):
                 for a in range(2):
                     codes, plane = tap_q[a, b]
@@ -248,89 +280,103 @@ def tile_list_slate_cleavage_board_kernel(
             nc.scalar.activation(whole[:], prod[:], ACT.Copy, scale=0.5 / math.pi, bias=ROUNDER)
             nc.scalar.activation(u[:], prod[:], ACT.Copy, scale=0.5 / math.pi)
             nc.scalar.activation(minus_whole[:], whole[:], ACT.Copy, scale=-1.0, bias=ROUNDER)
-            frac = bank()
+            frac = bank("turned")
             for jb in range(PACK):
                 nc.tensor.matmul(frac[:, cols(jb)], u[:, cols(jb)], ident[:], start=True, stop=False, is_transpose=True)
                 nc.tensor.matmul(frac[:, cols(jb)], minus_whole[:, cols(jb)], ident[:], start=False, stop=True, is_transpose=True)
             turns[b, t] = frac
 
         def make_h1(b, t):
-            nc.scalar.activation(gated[b][:, t, :], wg1_sb[:, t, :], ACT.Copy, scale=channel(0, b, t))
-            sines[b, t] = ring.tile([P, S], F32, name="sine", bufs=3)
+            sines[b, t] = slot("h7" if t % 2 == 0 else "s0" if (b, t) == (0, 1) else "w1", [P, S], F32, "sine")
             nc.scalar.activation(sines[b, t][:], turns[b, t][:], ACT.Sin, scale=2.0 * math.pi)
 
         def put_h1(b, t):
             nc.vector.tensor_tensor(pages[b, t][:].indirect(idx3[:]), sines[b, t][:], gated[b][:, t, :], ALU.mult)
 
-        x_tag = {(0, 0): "s3", (0, 1): "s4", (1, 0): "s5", (1, 1): "s2"}
-        xs, rested, x_q = {}, {}, {}
+        x_tag = {0: "s3", 2: "s4", 4: "s5", 6: "s8"}
+        rested_tag = {0: "s7", 1: "s0"}
+        pairs, xs, rested, grouped_x, x_q = {}, {}, {}, {}, {}
+        last = len(tiles) - 1
 
-        def fetch(b, t, h):
+        def half(h):
+            return slice(h * S, (h + 1) * S)
+
+        def fetch(i):
+            if i % 2 == 0:
+                pairs[i] = slot(x_tag[i], [P, 2, 2 * S], F32, "x%d" % i)
+            xs[i] = pairs[i - i % 2][:, i % 2, :]
+            page = pages[tiles[i]]
+            if i < last:
+                nc.vector.tensor_copy(xs[i], page[:].indirect(idx5[:]))
+            else:
+                for h in range(2):
+                    nc.vector.tensor_copy(xs[i][:, half(h)], page[:].indirect(idx5[:, 32 * h : 32 * (h + 1)]))
+
+        def add_rest(i):
+            b, t = tiles[i]
             if t == 0:
-                xs[b, h] = slot(x_tag[b, h], [P, PACK, S], F32, "x%d%d" % (b, h))
-            nc.vector.tensor_copy(xs[b, h][:, t, :], pages[b, t][:].indirect(idx5[:, 32 * h : 32 * (h + 1)]))
+                rested[b] = slot(rested_tag[b], [P, PACK, 2 * S], BF16, "rested%d" % b)
+            nc.scalar.activation(rested[b][:, t, :], xs[i], ACT.Identity, bias=channel(1, b, t))
 
-        def add_rest(b, t, h):
-            if t == 0:
-                rested[b, h] = ring.tile([P, PACK, S], BF16, name="rested")
-            nc.scalar.activation(rested[b, h][:, t, :], xs[b, h][:, t, :], ACT.Identity, bias=channel(1, b, t))
+        def take_abs(ap):
+            nc.scalar.activation(ap, ap, ACT.Abs)
 
-        def take_abs(b, t, h):
-            nc.scalar.activation(xs[b, h][:, t, :], xs[b, h][:, t, :], ACT.Abs)
+        def interleave(b, h, count):
+            grouped_x[b, h] = slot(("g2", "g3", "h1", "g2")[2 * b + h], [P, S * PACK], BF16, "grouped_x")
+            nc.scalar.copy(
+                grouped_x[b, h][:].rearrange("p (c i t) -> p c t i", i=4, t=PACK)[:, :, 0:count, :],
+                rested[b][:, 0:count, half(h)].rearrange("p t (c i) -> p c t i", i=4),
+            )
 
         def quantise_x(b, h):
-            grouped = ring.tile([P, S * PACK], BF16, name="grouped", tag="grouped", bufs=3, align_bytes=64)
-            nc.scalar.copy(
-                grouped[:].rearrange("p (c i t) -> p c t i", i=4, t=PACK),
-                rested[b, h][:].rearrange("p t (c i) -> p c t i", i=4),
-            )
-            x_q[b, h] = quantise(grouped, "x%d%d" % (b, h))
+            x_q[b, h] = quantise(grouped_x[b, h], "x%d%d" % (b, h))
 
-        tap_q[0, 1] = quantise(round_weight(nc.scalar.copy, tap_raw[0, 1]), "tap01")
-        put_h2(1, 2)
-        tap_q[1, 1] = quantise(round_weight(nc.scalar.copy, tap_raw[1, 1]), "tap11")
-        put_h2(1, 3)
-        for i in range(3):
+        for i in range(2):
             tap_product(*tiles[i])
+        put_h2(6)
+        read_plane = deal_plane(read_plane_raw, "read_plane", "h6")
+        put_h2(7)
         make_h1(0, 0)
+        tap_product(*tiles[2])
 
-        read_words = slot("s6", [P, 2 * H], I32, "read_words")
+        read_words = slot("w3", [P, 2 * H], I32, "read_words")
         nc.vector.tensor_copy(
             read_words[:].rearrange("p (g t mo mi) -> p g mo t mi", g=2 * NB, t=PACK, mi=4),
             read_raw[:].rearrange("p (g mo mi t) -> p g mo t mi", g=2 * NB, t=PACK, mi=4),
         )
-        read_plane = deal_plane(read_plane_raw, "read_plane")
-
-        def after_fetch(i):
-            b, t = tiles[i]
-            for h in range(2 - b):
-                add_rest(b, t, h)
-            for h in range(2 - b):
-                if t == PACK - 1:
-                    quantise_x(b, h)
-                take_abs(b, t, h)
 
         for i, (b, t) in enumerate(tiles):
             if i + 1 < len(tiles):
                 make_h1(*tiles[i + 1])
             put_h1(b, t)
-            for h in range(2 - b):
-                fetch(b, t, h)
+            fetch(i)
+            if i < 2:
+                tap_q[i, 1] = quantise(tap_grouped[i, 1], "tap%d1" % i, "page0%d" % i)
             if i + 3 < len(tiles):
                 tap_product(*tiles[i + 3])
             if i >= 1:
-                after_fetch(i - 1)
-        for t in range(PACK):
-            fetch(1, t, 1)
-        after_fetch(len(tiles) - 1)
-        for t in range(PACK):
-            add_rest(1, t, 1)
+                add_rest(i - 1)
+            if i in (PACK + 1, PACK + 2):
+                interleave(0, i - PACK - 1, PACK)
+                quantise_x(0, i - PACK - 1)
+            if b == 1 and i < last:
+                take_abs(xs[2 * t])
+                take_abs(xs[2 * t + 1])
+
+        def finish_x(h):
+            interleave(1, h, PACK - 1)
+            nc.scalar.activation(
+                grouped_x[1, h][:].rearrange("p (j t) -> p t j", t=PACK)[:, PACK - 1, :],
+                xs[last][:, half(h)], ACT.Identity, bias=channel(1, *tiles[last]),
+            )
+            quantise_x(1, h)
+            take_abs(xs[last][:, half(h)])
 
         out_rows = out.rearrange("(b p t) j -> b t p j", b=NB, t=PACK)
 
-        def finish(b, t, h):
-            c = b * PACK + t
-            y = bank()
+        def finish(c, h):
+            b, t = tiles[c]
+            y = bank(("tint", "line", "tap", "turned")[c % 4])
             for a in range(2):
                 codes, plane = x_q[a, h]
                 nc.tensor.matmul_mx(
@@ -340,16 +386,16 @@ def tile_list_slate_cleavage_board_kernel(
                     rhs=codes[:].bitcast(FP8X4), rhs_scale=plane[:],
                     start=(a == 0), stop=(a == 1),
                 )
-            res = xs[b, h][:, t, :]
+            res = xs[c][:, half(h)]
             nc.vector.scalar_tensor_tensor(res, res, channel(2, b, t), y[:], ALU.mult, ALU.add)
             nc.sync.dma_start(out_rows[b, t][:, h * S : (h + 1) * S], res)
 
-        for b, t in tiles[:PACK]:
-            finish(b, t, 0)
-        quantise_x(1, 1)
-        for t in range(PACK):
-            take_abs(1, t, 1)
-        for b, t in tiles[PACK:]:
-            finish(b, t, 0)
-        for b, t in tiles:
-            finish(b, t, 1)
+        finish_x(0)
+        take_abs(xs[last - 1])
+        for c in range(PACK):
+            finish(c, 0)
+        finish_x(1)
+        for c in range(PACK, len(tiles)):
+            finish(c, 0)
+        for c in range(len(tiles)):
+            finish(c, 1)

@@ -49,7 +49,7 @@ def tile_list_slate_cleavage_board_kernel(
             return keep.tile(shape, dtype, name=name, tag=tag, align_bytes=64)
 
         def zeroed_plane(engine, width, name):
-            plane = keep.tile([P, width], U8, name=name, align_bytes=64)
+            plane = slot(name, [P, width], U8, name)
             engine.memset(plane[:].bitcast(I32), 0)
             return plane
 
@@ -163,21 +163,6 @@ def tile_list_slate_cleavage_board_kernel(
         for v, vec in enumerate((gain, rest, lift)):
             nc.sync.dma_start(vec_rows[NB * v : NB * (v + 1), :], vec.rearrange("(b c) -> b c", b=NB))
         wg1_rows = load_rows(wg1, "wg1_rows", "wg_rows")
-        pages[0, 1] = load_page(0, 1)
-        v_all = [load_words("s3", tab_words[0], "v_all0"), load_words("s4", tab_words[1], "v_all1")]
-        pages[0, 2] = load_page(0, 2)
-        line_raw[1] = load_weight("s2", w_line, 0, 1, "line_raw1")
-        pages[0, 3] = load_page(0, 3)
-        tap_raw = {(a, 0): load_weight("s%d" % (5 + a), w_tap, a, 0, "tap_raw%d0" % a) for a in range(2)}
-        tap_raw[0, 1] = load_weight("s7", w_tap, 0, 1, "tap_raw01")
-        tap_raw[1, 1] = load_weight("s8", w_tap, 1, 1, "tap_raw11")
-        pages[1, 0] = load_page(1, 0)
-        pages[1, 1] = load_page(1, 1)
-        load_scale_rows(nc.sync, read_plane_raw, w_read_scales)
-        pages[1, 2] = load_page(1, 2)
-        idx3 = load_list(offs3, "idx3")
-        idx5 = load_list(offs5, "idx5")
-
         wg2_dealt = []
         tint_words = slot("g1", [P, 2 * H], U8, "tint_words")
         for b in range(NB):
@@ -192,9 +177,26 @@ def tile_list_slate_cleavage_board_kernel(
         line_q = {0: quantise(line_grouped, "line0")}
         v2_words = gather(U32, v2_all, idx2, "v2_words")
 
+        v_all, tap_raw = {}, {}
+        pages[0, 1] = load_page(0, 1)
+        v_all[0] = load_words("s3", tab_words[0], "v_all0")
+        pages[0, 2] = load_page(0, 2)
+        line_raw[1] = load_weight("s2", w_line, 0, 1, "line_raw1")
+        pages[0, 3] = load_page(0, 3)
+        v_all[1] = load_words("s4", tab_words[1], "v_all1")
+        tap_raw[0, 0] = load_weight("s5", w_tap, 0, 0, "tap_raw00")
+        tap_raw[1, 0] = load_weight("s6", w_tap, 1, 0, "tap_raw10")
+        pages[1, 0] = load_page(1, 0)
+        pages[1, 1] = load_page(1, 1)
+        load_scale_rows(nc.sync, read_plane_raw, w_read_scales)
+        idx3 = load_list(offs3, "idx3")
+        idx5 = load_list(offs5, "idx5")
+        pages[1, 2] = load_page(1, 2)
+        tap_raw[0, 1] = load_weight("s7", w_tap, 0, 1, "tap_raw01")
+        tap_raw[1, 1] = load_weight("s8", w_tap, 1, 1, "tap_raw11")
+        pages[1, 3] = load_page(1, 3)
         read_raw = slot("s0", [P, 2 * H], I32, "read_raw")
         nc.sync.dma_start(read_raw[:].rearrange("p (a c) -> p a c", a=2), w_read_words.rearrange("a p c i -> p a (c i)").bitcast(I32))
-        pages[1, 3] = load_page(1, 3)
 
         h2 = []
 
@@ -230,11 +232,10 @@ def tile_list_slate_cleavage_board_kernel(
         put_h2(1)
         for c in range(2, len(tiles)):
             start_h2(c)
-        v_words = [gather(U32, v_all[0], idx, "v_words0", "h0")]
         put_h2(2)
         put_h2(3)
         line_q[1] = quantise(round_weight(nc.scalar.copy, line_raw[1], "g1"), "line1", "h3")
-        v_words.append(gather(U32, v_all[1], idx, "v_words1", "g1"))
+        v_words = [gather(U32, v_all[a], idx, "v_words%d" % a, ("g1", "h0")[a]) for a in range(2)]
         tap_grouped = {
             (a, b): round_weight(nc.scalar.copy, tap_raw[a, b], (("g3", "g2"), ("h1", "h2"))[b][a])
             for b in range(NB) for a in range(2)
@@ -287,14 +288,14 @@ def tile_list_slate_cleavage_board_kernel(
             turns[b, t] = frac
 
         def make_h1(b, t):
-            sines[b, t] = slot("h7" if t % 2 == 0 else "s0" if (b, t) == (0, 1) else "w1", [P, S], F32, "sine")
+            sines[b, t] = slot("h6" if t % 2 == 0 else "read_plane_raw", [P, S], F32, "sine")
             nc.scalar.activation(sines[b, t][:], turns[b, t][:], ACT.Sin, scale=2.0 * math.pi)
 
         def put_h1(b, t):
             nc.vector.tensor_tensor(pages[b, t][:].indirect(idx3[:]), sines[b, t][:], gated[b][:, t, :], ALU.mult)
 
         x_tag = {0: "s3", 2: "s4", 4: "s5", 6: "s8"}
-        rested_tag = {0: "s7", 1: "s0"}
+        rested_tag = {0: "s7", 1: "s2"}
         pairs, xs, rested, grouped_x, x_q = {}, {}, {}, {}, {}
         last = len(tiles) - 1
 
@@ -328,40 +329,48 @@ def tile_list_slate_cleavage_board_kernel(
                 rested[b][:, 0:count, half(h)].rearrange("p t (c i) -> p c t i", i=4),
             )
 
-        def quantise_x(b, h):
-            x_q[b, h] = quantise(grouped_x[b, h], "x%d%d" % (b, h))
+        def quantise_x(b, h, tag=None):
+            x_q[b, h] = quantise(grouped_x[b, h], "x%d%d" % (b, h), tag)
+
+        def deal_read_words(a, tag):
+            dealt = slot(tag, [P, H], I32, "read_words%d" % a)
+            nc.vector.tensor_copy(
+                dealt[:].rearrange("p (b t mo mi) -> p b mo t mi", b=NB, t=PACK, mi=4),
+                read_raw[:, a * H : (a + 1) * H].rearrange("p (b mo mi t) -> p b mo t mi", b=NB, t=PACK, mi=4),
+            )
+            return dealt
 
         for i in range(2):
             tap_product(*tiles[i])
         put_h2(6)
-        read_plane = deal_plane(read_plane_raw, "read_plane", "h6")
+        read_plane = deal_plane(read_plane_raw, "read_plane", "w2")
         put_h2(7)
         make_h1(0, 0)
         tap_product(*tiles[2])
-
-        read_words = slot("w3", [P, 2 * H], I32, "read_words")
-        nc.vector.tensor_copy(
-            read_words[:].rearrange("p (g t mo mi) -> p g mo t mi", g=2 * NB, t=PACK, mi=4),
-            read_raw[:].rearrange("p (g mo mi t) -> p g mo t mi", g=2 * NB, t=PACK, mi=4),
-        )
 
         for i, (b, t) in enumerate(tiles):
             if i + 1 < len(tiles):
                 make_h1(*tiles[i + 1])
             put_h1(b, t)
             fetch(i)
-            if i < 2:
-                tap_q[i, 1] = quantise(tap_grouped[i, 1], "tap%d1" % i, "page0%d" % i)
+            if i == 0:
+                tap_q[0, 1] = quantise(tap_grouped[0, 1], "tap01", "page00")
+            if i == 1:
+                tap_q[1, 1] = quantise(tap_grouped[1, 1], "tap11", "page01")
+            if i == 2:
+                read_words = [deal_read_words(0, "page02")]
             if i + 3 < len(tiles):
                 tap_product(*tiles[i + 3])
             if i >= 1:
                 add_rest(i - 1)
-            if i in (PACK + 1, PACK + 2):
-                interleave(0, i - PACK - 1, PACK)
-                quantise_x(0, i - PACK - 1)
-            if b == 1 and i < last:
-                take_abs(xs[2 * t])
-                take_abs(xs[2 * t + 1])
+                if i < last:
+                    take_abs(xs[i - 1])
+            if i in (PACK, PACK + 1):
+                interleave(0, i - PACK, PACK)
+            if i == PACK:
+                quantise_x(0, 0)
+
+        read_words.append(deal_read_words(1, "s1"))
 
         def finish_x(h):
             interleave(1, h, PACK - 1)
@@ -369,7 +378,6 @@ def tile_list_slate_cleavage_board_kernel(
                 grouped_x[1, h][:].rearrange("p (j t) -> p t j", t=PACK)[:, PACK - 1, :],
                 xs[last][:, half(h)], ACT.Identity, bias=channel(1, *tiles[last]),
             )
-            quantise_x(1, h)
             take_abs(xs[last][:, half(h)])
 
         out_rows = out.rearrange("(b p t) j -> b t p j", b=NB, t=PACK)
@@ -381,7 +389,7 @@ def tile_list_slate_cleavage_board_kernel(
                 codes, plane = x_q[a, h]
                 nc.tensor.matmul_mx(
                     out=y[:],
-                    lhsT=read_words[:, a * H + c * P : a * H + (c + 1) * P].bitcast(FP8X4),
+                    lhsT=read_words[a][:, cols(c)].bitcast(FP8X4),
                     lhsT_scale=read_plane[4 * a : P, cols(c)],
                     rhs=codes[:].bitcast(FP8X4), rhs_scale=plane[:],
                     start=(a == 0), stop=(a == 1),
@@ -391,11 +399,13 @@ def tile_list_slate_cleavage_board_kernel(
             nc.sync.dma_start(out_rows[b, t][:, h * S : (h + 1) * S], res)
 
         finish_x(0)
+        quantise_x(1, 0)
+        quantise_x(0, 1, "h1")
         take_abs(xs[last - 1])
-        for c in range(PACK):
-            finish(c, 0)
         finish_x(1)
-        for c in range(PACK, len(tiles)):
+        for c in range(len(tiles)):
+            if c == last - 1:
+                quantise_x(1, 1)
             finish(c, 0)
         for c in range(len(tiles)):
             finish(c, 1)

@@ -106,8 +106,8 @@ def tile_list_slate_cleavage_board_kernel(
         def round_weight(copy, raw, tag):
             grouped = slot(tag, [P, BLK * PACK], BF16, "grouped")
             copy(
-                grouped[:].rearrange("p (t m j) -> p m t j", t=PACK, j=PACK),
-                raw[:].rearrange("p j (m t) -> p m t j", t=PACK),
+                grouped[:].rearrange("p (t m j) -> p m j t", t=PACK, j=PACK),
+                raw[:].rearrange("p j (m t) -> p m j t", t=PACK),
             )
             return grouped
 
@@ -179,21 +179,21 @@ def tile_list_slate_cleavage_board_kernel(
 
         v_all, tap_raw = {}, {}
         pages[0, 1] = load_page(0, 1)
-        v_all[0] = load_words("s3", tab_words[0], "v_all0")
-        pages[0, 2] = load_page(0, 2)
         line_raw[1] = load_weight("s2", w_line, 0, 1, "line_raw1")
+        pages[0, 2] = load_page(0, 2)
+        v_all[0] = load_words("s3", tab_words[0], "v_all0")
         pages[0, 3] = load_page(0, 3)
         v_all[1] = load_words("s4", tab_words[1], "v_all1")
         tap_raw[0, 0] = load_weight("s5", w_tap, 0, 0, "tap_raw00")
         tap_raw[1, 0] = load_weight("s6", w_tap, 1, 0, "tap_raw10")
+        tap_raw[0, 1] = load_weight("s7", w_tap, 0, 1, "tap_raw01")
         pages[1, 0] = load_page(1, 0)
+        tap_raw[1, 1] = load_weight("s8", w_tap, 1, 1, "tap_raw11")
         pages[1, 1] = load_page(1, 1)
         load_scale_rows(nc.sync, read_plane_raw, w_read_scales)
         idx3 = load_list(offs3, "idx3")
         idx5 = load_list(offs5, "idx5")
         pages[1, 2] = load_page(1, 2)
-        tap_raw[0, 1] = load_weight("s7", w_tap, 0, 1, "tap_raw01")
-        tap_raw[1, 1] = load_weight("s8", w_tap, 1, 1, "tap_raw11")
         pages[1, 3] = load_page(1, 3)
         read_raw = slot("s0", [P, 2 * H], I32, "read_raw")
         nc.sync.dma_start(read_raw[:].rearrange("p (a c) -> p a c", a=2), w_read_words.rearrange("a p c i -> p a (c i)").bitcast(I32))
@@ -288,7 +288,7 @@ def tile_list_slate_cleavage_board_kernel(
             turns[b, t] = frac
 
         def make_h1(b, t):
-            sines[b, t] = slot("h6" if t % 2 == 0 else "read_plane_raw", [P, S], F32, "sine")
+            sines[b, t] = slot("h7" if t % 2 == 0 else "read_plane_raw", [P, S], F32, "sine")
             nc.scalar.activation(sines[b, t][:], turns[b, t][:], ACT.Sin, scale=2.0 * math.pi)
 
         def put_h1(b, t):
@@ -343,8 +343,8 @@ def tile_list_slate_cleavage_board_kernel(
         for i in range(2):
             tap_product(*tiles[i])
         put_h2(6)
-        read_plane = deal_plane(read_plane_raw, "read_plane", "w2")
         put_h2(7)
+        read_plane = deal_plane(read_plane_raw, "read_plane", "w3")
         make_h1(0, 0)
         tap_product(*tiles[2])
 

@@ -22,7 +22,12 @@ SLOTS = 2048
 S = 512
 H = 1024
 NB = H // BLK
+TAP_PASSES = 2
 QUADS = 4
+LINE = 16
+ROW_TILES = [(b, t) for b in range(NB) for t in range(PACK)]
+LAST = len(ROW_TILES) - 1
+GAIN, REST, LIFT = range(3)
 ROUNDER = 12582912.0
 
 FLOPS = 4294967296
@@ -39,47 +44,59 @@ def tile_list_slate_cleavage_board_kernel(
         keep = ctx.enter_context(tc.tile_pool(name="keep", bufs=1))
         ring = ctx.enter_context(tc.tile_pool(name="ring", bufs=2))
         psum = ctx.enter_context(tc.psum_pool(name="psum", bufs=2))
+        home = {}
+
+        def sbuf(name, shape, dtype, on=None):
+            home[name] = home[on] if on else name
+            return keep.tile(shape, dtype, name=name, tag=home[name], align_bytes=64)
+
+        def bank(tag):
+            return psum.tile([P, S], F32, name=tag, tag=tag)
+
+        def cols(n):
+            return slice(n * P, (n + 1) * P)
+
+        def half(h):
+            return slice(h * S, (h + 1) * S)
 
         def load_list(src, name):
             tile = lists.tile(list(src.shape), U16, name=name)
             nc.sync.dma_start(tile[:], src)
             return tile
 
-        def slot(tag, shape, dtype, name):
-            return keep.tile(shape, dtype, name=name, tag=tag, align_bytes=64)
-
-        def zeroed_plane(engine, width, name):
-            plane = slot(name, [P, width], U8, name)
+        def zeroed_plane(engine, name, width):
+            plane = sbuf(name, [P, width], U8)
             engine.memset(plane[:].bitcast(I32), 0)
             return plane
 
-        def load_scale_rows(queue, plane, scales):
+        def load_scale_rows(plane, scales):
             rows = 4 * scales.shape[0]
             for q in range(QUADS):
-                queue.dma_start(
+                nc.sync.dma_start(
                     plane[32 * q : 32 * q + rows, :].bitcast(I32),
                     scales[:, 4 * q : 4 * q + 4, :].bitcast(I32),
                 )
 
-        def load_words(tag, words, name):
-            tile = slot(tag, [P, SLOTS], U32, name)
+        def load_table(words, name):
+            tile = sbuf(name, [P, SLOTS], U32)
             nc.sync.dma_start(tile[:].bitcast(I32), words.rearrange("p t i -> p (t i)").bitcast(I32))
             return tile
 
-        def load_weight(tag, w, a, b, name):
-            raw = slot(tag, [P, PACK, BLK], F32, name)
+        def load_weight(w, a, b, name):
+            raw = sbuf(name, [P, PACK, BLK], F32)
             rows = w[a * BLK : (a + 1) * BLK, b * BLK : (b + 1) * BLK]
             nc.sync.dma_start(raw[:], rows.rearrange("(p j) c -> p j c", j=PACK))
             return raw
 
-        def load_page(b, t):
-            name = "page%d%d" % (b, t)
-            page = slot("s1" if (b, t) == (1, 3) else name, [P, SLOTS], F32, name)
-            nc.sync.dma_start(page[:], page0.rearrange("(b p t) s -> b t p s", b=NB, t=PACK)[b, t])
-            return page
+        pages = {}
 
-        def load_rows(wg, name, tag):
-            tile = slot(tag, [P, S], F32, name)
+        def load_page(c, on=None):
+            b, t = ROW_TILES[c]
+            pages[c] = sbuf("page%d" % c, [P, SLOTS], F32, on)
+            nc.sync.dma_start(pages[c][:], page0.rearrange("(b p t) s -> b t p s", b=NB, t=PACK)[b, t])
+
+        def load_rows(wg, name, on=None):
+            tile = sbuf(name, [P, S], F32, on)
             nc.sync.dma_start(tile[:], wg)
             return tile
 
@@ -98,160 +115,161 @@ def tile_list_slate_cleavage_board_kernel(
             )
             return turn(picked, "turned")
 
-        def gather(dtype, window, offsets, name, tag=None):
-            picked = slot(tag or name, [P, S], dtype, name)
+        def gather(window, offsets, dtype, name, on=None):
+            picked = sbuf(name, [P, S], dtype, on)
             nc.vector.tensor_copy(picked[:], window[:].indirect(offsets[:]))
             return picked
 
-        def round_weight(copy, raw, tag):
-            grouped = slot(tag, [P, BLK * PACK], BF16, "grouped")
+        def round_weight(copy, raw, name, on=None):
+            grouped = sbuf(name, [P, BLK * PACK], BF16, on)
             copy(
                 grouped[:].rearrange("p (t m j) -> p m j t", t=PACK, j=PACK),
                 raw[:].rearrange("p j (m t) -> p m j t", t=PACK),
             )
             return grouped
 
-        def quantise(grouped, name, tag=None):
-            codes = slot(tag or name, [P, BLK], U32, name + "_codes")
-            plane = keep.tile([P, BLK], U8, name=name + "_plane", align_bytes=64)
+        def quantise(grouped, name, on=None):
+            codes = sbuf(name + "_codes", [P, BLK], U32, on)
+            plane = sbuf(name + "_plane", [P, BLK], U8)
             nc.vector.quantize_mx(out=codes[:].bitcast(FP8X4), scales=plane[:], in_=grouped[:])
             return codes, plane
 
-        def deal_plane(plane, name, tag):
-            dealt = slot(tag, [P, H], U8, name)
+        def deal_plane(plane, name, on=None):
+            dealt = sbuf(name, [P, H], U8, on)
             nc.vector.tensor_copy(
-                dealt[:].rearrange("p (b t mo mi) -> p b mo t mi", b=NB, t=PACK, mi=16),
-                plane[:].rearrange("p (b mo mi t) -> p b mo t mi", b=NB, t=PACK, mi=16),
+                dealt[:].rearrange("p (b t mo mi) -> p b mo t mi", b=NB, t=PACK, mi=LINE),
+                plane[:].rearrange("p (b mo mi t) -> p b mo t mi", b=NB, t=PACK, mi=LINE),
             )
             return dealt
 
-        def bank(tag):
-            return psum.tile([P, S], F32, name=tag, tag=tag)
-
-        def cols(t):
-            return slice(t * P, (t + 1) * P)
-
-        tiles = [(b, t) for b in range(NB) for t in range(PACK)]
-
         ident = keep.tile([P, P], F32, name="ident")
         make_identity(nc, ident[:])
-        v2_plane_all = zeroed_plane(nc.vector, SLOTS, "v2_plane_all")
-        v_plane_all = zeroed_plane(nc.gpsimd, SLOTS, "v_plane_all")
-        read_plane_raw = zeroed_plane(nc.gpsimd, H, "read_plane_raw")
+        v2_plane_all = zeroed_plane(nc.vector, "v2_plane_all", SLOTS)
+        v_plane_all = zeroed_plane(nc.gpsimd, "v_plane_all", SLOTS)
+        read_plane_raw = zeroed_plane(nc.gpsimd, "read_plane_raw", H)
         vec_rows = keep.tile([P, BLK], F32, name="vec_rows")
         nc.gpsimd.memset(vec_rows[:], 0.0)
 
         idx2 = load_list(offs2, "idx2")
-        wg2_rows = load_rows(wg2, "wg2_rows", "wg_rows")
-        tint_plane_raw = keep.tile([P, H], U8, name="tint_plane_raw", align_bytes=64)
+        tint_plane_raw = sbuf("tint_plane_raw", [P, H], U8)
         for q in range(QUADS):
             rows = w_tint_scales[0, 4 * q : 4 * q + 4, :].bitcast(I32)
             nc.sync.dma_start(
                 tint_plane_raw[32 * q : 32 * q + 32, :].bitcast(I32),
                 rows.unsqueeze(0).broadcast_to([8, 4, H // 4]),
             )
-        tint_raw = keep.tile([P, 2 * H], U8, name="tint_raw", align_bytes=64)
+        tint_raw = sbuf("tint_raw", [P, 2 * H], U8)
         nc.sync.dma_start(tint_raw[:].bitcast(I32), w_tint_words[0].bitcast(I32))
-        line_raw = {0: load_weight("s1", w_line, 0, 0, "line_raw0")}
-        load_scale_rows(nc.sync, v2_plane_all, tab2_scales)
-        v2_all = load_words("s0", tab2_words[0], "v2_all")
+        wg2_rows = load_rows(wg2, "wg2_rows")
+        line_raw = [load_weight(w_line, 0, 0, "line_raw0")]
+        load_scale_rows(v2_plane_all, tab2_scales)
+        v2_all = load_table(tab2_words[0], "v2_all")
         idx4 = load_list(offs4, "idx4")
-        load_scale_rows(nc.sync, v_plane_all, tab_scales)
+        load_scale_rows(v_plane_all, tab_scales)
         idx = load_list(offs, "idx")
-        pages = {(0, 0): load_page(0, 0)}
+        load_page(0)
         wg2_turned = turn(wg2_rows, "tap")
         for v, vec in enumerate((gain, rest, lift)):
             nc.sync.dma_start(vec_rows[NB * v : NB * (v + 1), :], vec.rearrange("(b c) -> b c", b=NB))
-        wg1_rows = load_rows(wg1, "wg1_rows", "wg_rows")
-        wg2_dealt = []
-        tint_words = slot("g1", [P, 2 * H], U8, "tint_words")
-        for b in range(NB):
-            half = slice(b * 2 * BLK, (b + 1) * 2 * BLK)
-            nc.vector.tensor_copy(
-                tint_words[:, half].rearrange("p (t mo mi e) -> p mo t mi e", t=PACK, mi=8, e=2),
-                tint_raw[:, half].rearrange("p (mo mi t e) -> p mo t mi e", t=PACK, mi=8, e=2),
-            )
-        tint_plane = deal_plane(tint_plane_raw, "tint_plane", "g3")
-        line_grouped = round_weight(nc.vector.tensor_copy, line_raw[0], "g2")
-        v2_plane = gather(U8, v2_plane_all, idx2, "v2_plane")
-        line_q = {0: quantise(line_grouped, "line0")}
-        v2_words = gather(U32, v2_all, idx2, "v2_words")
+        wg1_rows = load_rows(wg1, "wg1_rows", on="wg2_rows")
 
-        v_all, tap_raw = {}, {}
-        pages[0, 1] = load_page(0, 1)
-        line_raw[1] = load_weight("s2", w_line, 0, 1, "line_raw1")
-        pages[0, 2] = load_page(0, 2)
-        v_all[0] = load_words("s3", tab_words[0], "v_all0")
-        pages[0, 3] = load_page(0, 3)
-        v_all[1] = load_words("s4", tab_words[1], "v_all1")
-        tap_raw[0, 0] = load_weight("s5", w_tap, 0, 0, "tap_raw00")
-        tap_raw[1, 0] = load_weight("s6", w_tap, 1, 0, "tap_raw10")
-        tap_raw[0, 1] = load_weight("s7", w_tap, 0, 1, "tap_raw01")
-        pages[1, 0] = load_page(1, 0)
-        tap_raw[1, 1] = load_weight("s8", w_tap, 1, 1, "tap_raw11")
-        pages[1, 1] = load_page(1, 1)
-        load_scale_rows(nc.sync, read_plane_raw, w_read_scales)
+        tint_words = sbuf("tint_words", [P, 2 * H], U8)
+        for b in range(NB):
+            run = slice(b * 2 * BLK, (b + 1) * 2 * BLK)
+            nc.vector.tensor_copy(
+                tint_words[:, run].rearrange("p (t mo mi e) -> p mo t mi e", t=PACK, mi=LINE // 2, e=2),
+                tint_raw[:, run].rearrange("p (mo mi t e) -> p mo t mi e", t=PACK, mi=LINE // 2, e=2),
+            )
+        tint_plane = deal_plane(tint_plane_raw, "tint_plane")
+        line_grouped = round_weight(nc.vector.tensor_copy, line_raw[0], "line_grouped0")
+        v2_plane = gather(v2_plane_all, idx2, U8, "v2_plane")
+        line_q = [quantise(line_grouped, "line0")]
+        v2_words = gather(v2_all, idx2, U32, "v2_words")
+
+        load_page(1)
+        line_raw.append(load_weight(w_line, 0, 1, "line_raw1"))
+        load_page(2)
+        v_all = [load_table(tab_words[0], "v_all0")]
+        load_page(3)
+        v_all.append(load_table(tab_words[1], "v_all1"))
+        tap_raw = {}
+        for a, b in ((0, 0), (1, 0), (0, 1)):
+            tap_raw[a, b] = load_weight(w_tap, a, b, "tap_raw%d%d" % (a, b))
+        load_page(4)
+        tap_raw[1, 1] = load_weight(w_tap, 1, 1, "tap_raw11")
+        load_page(5)
+        load_scale_rows(read_plane_raw, w_read_scales)
         idx3 = load_list(offs3, "idx3")
         idx5 = load_list(offs5, "idx5")
-        pages[1, 2] = load_page(1, 2)
-        pages[1, 3] = load_page(1, 3)
-        read_raw = slot("s0", [P, 2 * H], I32, "read_raw")
-        nc.sync.dma_start(read_raw[:].rearrange("p (a c) -> p a c", a=2), w_read_words.rearrange("a p c i -> p a (c i)").bitcast(I32))
+        load_page(6)
+        load_page(7, on="line_raw0")
+        read_raw = sbuf("read_raw", [P, NB * H], I32, on="v2_all")
+        nc.sync.dma_start(
+            read_raw[:].rearrange("p (a c) -> p a c", a=NB),
+            w_read_words.rearrange("a p c i -> p a (c i)").bitcast(I32),
+        )
 
-        h2 = []
+        wg2_dealt, h2 = [], []
 
         def start_h2(c):
             if c < PACK:
-                wg2_dealt.append(slot("w%d" % c, [P, S], F32, "wg2_dealt%d" % c))
+                wg2_dealt.append(sbuf("wg2_dealt%d" % c, [P, S], F32))
                 nc.scalar.copy(wg2_dealt[c][:], deal_rows(wg2_turned, c)[:])
-            tint_ps = bank("tint")
+            tint = bank("tint")
             nc.tensor.matmul_mx(
-                out=tint_ps[:],
+                out=tint[:],
                 lhsT=tint_words[:, 2 * c * P : 2 * (c + 1) * P].bitcast(FP4X4), lhsT_scale=tint_plane[:, cols(c)],
                 rhs=v2_words[:].bitcast(FP8X4), rhs_scale=v2_plane[:], start=True, stop=True,
             )
-            h2.append(slot("h%d" % c, [P, S], F32, "h2_%d" % c))
-            nc.scalar.copy(h2[c][:], tint_ps[:])
+            h2.append(sbuf("h2_%d" % c, [P, S], F32))
+            nc.scalar.copy(h2[c][:], tint[:])
 
         def put_h2(c):
-            b, t = tiles[c]
-            line_ps = bank("line")
+            b, t = ROW_TILES[c]
+            line = bank("line")
             codes, plane = line_q[b]
             nc.tensor.matmul_mx(
-                out=line_ps[:],
+                out=line[:],
                 lhsT=codes[:, cols(t)].bitcast(FP8X4), lhsT_scale=plane[:, cols(t)],
                 rhs=v2_words[:].bitcast(FP8X4), rhs_scale=v2_plane[:], start=True, stop=True,
             )
-            nc.vector.tensor_tensor(h2[c][:], line_ps[:], h2[c][:], ALU.min)
-            nc.vector.tensor_tensor(pages[b, t][:].indirect(idx4[:]), h2[c][:], wg2_dealt[t][:], ALU.mult)
+            nc.vector.tensor_tensor(h2[c][:], line[:], h2[c][:], ALU.min)
+            nc.vector.tensor_tensor(pages[c][:].indirect(idx4[:]), h2[c][:], wg2_dealt[t][:], ALU.mult)
 
-        for c in range(2):
-            start_h2(c)
+        start_h2(0)
+        start_h2(1)
         put_h2(0)
-        v_plane = gather(U8, v_plane_all, idx, "v_plane")
+        v_plane = gather(v_plane_all, idx, U8, "v_plane")
         put_h2(1)
-        for c in range(2, len(tiles)):
+        for c in range(2, len(ROW_TILES)):
             start_h2(c)
         put_h2(2)
         put_h2(3)
-        line_q[1] = quantise(round_weight(nc.scalar.copy, line_raw[1], "g1"), "line1", "h3")
-        v_words = [gather(U32, v_all[a], idx, "v_words%d" % a, ("g1", "h0")[a]) for a in range(2)]
-        tap_grouped = {
-            (a, b): round_weight(nc.scalar.copy, tap_raw[a, b], (("g3", "g2"), ("h1", "h2"))[b][a])
-            for b in range(NB) for a in range(2)
-        }
+        line_grouped = round_weight(nc.scalar.copy, line_raw[1], "line_grouped1", on="tint_words")
+        line_q.append(quantise(line_grouped, "line1", on="h2_3"))
+        v_words = [
+            gather(v_all[0], idx, U32, "v_words0", on="line_grouped1"),
+            gather(v_all[1], idx, U32, "v_words1", on="h2_0"),
+        ]
+        tap_grouped = {}
+        for a, b, on in ((0, 0, "tint_plane"), (1, 0, "line_grouped0"), (0, 1, "h2_1"), (1, 1, "h2_2")):
+            tap_grouped[a, b] = round_weight(nc.scalar.copy, tap_raw[a, b], "tap_grouped%d%d" % (a, b), on)
 
-        vec_ps = bank("turned")
+        vec_bank = bank("turned")
         for t in range(PACK):
-            nc.tensor.transpose(vec_ps[:, cols(t)], vec_rows[:, t:BLK:PACK], ident[:])
-        vec_sb = keep.tile([P, PACK, 8], F32, name="vec_sb")
-        nc.scalar.copy(vec_sb[:], vec_ps[:].rearrange("p (t r) -> p t r", t=PACK)[:, :, 0:8])
+            nc.tensor.transpose(vec_bank[:, cols(t)], vec_rows[:, t:BLK:PACK], ident[:])
+        vec_cols = keep.tile([P, PACK, 3 * NB], F32, name="vec_cols")
+        nc.scalar.copy(vec_cols[:], vec_bank[:].rearrange("p (t r) -> p t r", t=PACK)[:, :, 0 : 3 * NB])
 
-        def channel(v, b, t):
-            return vec_sb[:, t, NB * v + b : NB * v + b + 1]
+        def channel(v, c):
+            b, t = ROW_TILES[c]
+            return vec_cols[:, t, NB * v + b : NB * v + b + 1]
 
         put_h2(4)
-        tap_q = {(a, 0): quantise(tap_grouped[a, 0], "tap%d0" % a, ("h4", "w0")[a]) for a in range(2)}
+        tap_q = {
+            (0, 0): quantise(tap_grouped[0, 0], "tap00", on="h2_4"),
+            (1, 0): quantise(tap_grouped[1, 0], "tap10", on="wg2_dealt0"),
+        }
         put_h2(5)
 
         gated = [keep.tile([P, PACK, S], F32, name="gated%d" % b) for b in range(NB)]
@@ -259,153 +277,148 @@ def tile_list_slate_cleavage_board_kernel(
         for t in range(PACK):
             dealt = deal_rows(wg1_turned, t)
             for b in range(NB):
-                nc.scalar.activation(gated[b][:, t, :], dealt[:], ACT.Copy, scale=channel(0, b, t))
-        sines = {}
+                nc.scalar.activation(gated[b][:, t, :], dealt[:], ACT.Copy, scale=channel(GAIN, b * PACK + t))
 
-        turns = {}
+        fractions, sines = {}, {}
 
-        def tap_product(b, t):
-            prod = bank("tap")
+        def tap_product(c):
+            b, t = ROW_TILES[c]
+            product = bank("tap")
             for jb in range(PACK):
-                for a in range(2):
+                for a in range(TAP_PASSES):
                     codes, plane = tap_q[a, b]
                     nc.tensor.matmul_mx(
-                        out=prod[:, cols(jb)],
+                        out=product[:, cols(jb)],
                         lhsT=v_words[a][:, cols(jb)].bitcast(FP8X4), lhsT_scale=v_plane[4 * a : P, cols(jb)],
                         rhs=codes[:, cols(t)].bitcast(FP8X4), rhs_scale=plane[:, cols(t)],
-                        start=(a == 0), stop=(a == 1),
+                        start=(a == 0), stop=(a == TAP_PASSES - 1),
                     )
-            u = ring.tile([P, S], F32, name="u")
+            turns = ring.tile([P, S], F32, name="turns")
             whole = ring.tile([P, S], U32, name="whole")
             minus_whole = ring.tile([P, S], F32, name="minus_whole")
-            nc.scalar.activation(whole[:], prod[:], ACT.Copy, scale=0.5 / math.pi, bias=ROUNDER)
-            nc.scalar.activation(u[:], prod[:], ACT.Copy, scale=0.5 / math.pi)
+            nc.scalar.activation(whole[:], product[:], ACT.Copy, scale=0.5 / math.pi, bias=ROUNDER)
+            nc.scalar.activation(turns[:], product[:], ACT.Copy, scale=0.5 / math.pi)
             nc.scalar.activation(minus_whole[:], whole[:], ACT.Copy, scale=-1.0, bias=ROUNDER)
-            frac = bank("turned")
+            fractions[c] = bank("turned")
             for jb in range(PACK):
-                nc.tensor.matmul(frac[:, cols(jb)], u[:, cols(jb)], ident[:], start=True, stop=False, is_transpose=True)
-                nc.tensor.matmul(frac[:, cols(jb)], minus_whole[:, cols(jb)], ident[:], start=False, stop=True, is_transpose=True)
-            turns[b, t] = frac
+                for term, first in ((turns, True), (minus_whole, False)):
+                    nc.tensor.matmul(
+                        fractions[c][:, cols(jb)], term[:, cols(jb)], ident[:],
+                        start=first, stop=not first, is_transpose=True,
+                    )
 
-        def make_h1(b, t):
-            sines[b, t] = slot("h7" if t % 2 == 0 else "read_plane_raw", [P, S], F32, "sine")
-            nc.scalar.activation(sines[b, t][:], turns[b, t][:], ACT.Sin, scale=2.0 * math.pi)
+        def make_sine(c):
+            sines[c] = sbuf("sine%d" % c, [P, S], F32, on=("h2_7", "read_plane_raw")[c % 2])
+            nc.scalar.activation(sines[c][:], fractions[c][:], ACT.Sin, scale=2.0 * math.pi)
 
-        def put_h1(b, t):
-            nc.vector.tensor_tensor(pages[b, t][:].indirect(idx3[:]), sines[b, t][:], gated[b][:, t, :], ALU.mult)
+        def put_h1(c):
+            b, t = ROW_TILES[c]
+            nc.vector.tensor_tensor(pages[c][:].indirect(idx3[:]), sines[c][:], gated[b][:, t, :], ALU.mult)
 
-        x_tag = {0: "s3", 2: "s4", 4: "s5", 6: "s8"}
-        rested_tag = {0: "s7", 1: "s2"}
-        pairs, xs, rested, grouped_x, x_q = {}, {}, {}, {}, {}
-        last = len(tiles) - 1
+        x_on = ("v_all0", "v_all1", "tap_raw00", "tap_raw11")
+        x_pairs, xs, rested, x_grouped, x_q = [], [], [], {}, {}
 
-        def half(h):
-            return slice(h * S, (h + 1) * S)
-
-        def fetch(i):
-            if i % 2 == 0:
-                pairs[i] = slot(x_tag[i], [P, 2, 2 * S], F32, "x%d" % i)
-            xs[i] = pairs[i - i % 2][:, i % 2, :]
-            page = pages[tiles[i]]
-            if i < last:
-                nc.vector.tensor_copy(xs[i], page[:].indirect(idx5[:]))
+        def fetch(c):
+            if c % 2 == 0:
+                x_pairs.append(sbuf("x%d" % c, [P, 2, 2 * S], F32, on=x_on[c // 2]))
+            xs.append(x_pairs[c // 2][:, c % 2, :])
+            if c < LAST:
+                nc.vector.tensor_copy(xs[c], pages[c][:].indirect(idx5[:]))
             else:
                 for h in range(2):
-                    nc.vector.tensor_copy(xs[i][:, half(h)], page[:].indirect(idx5[:, 32 * h : 32 * (h + 1)]))
+                    nc.vector.tensor_copy(xs[c][:, half(h)], pages[c][:].indirect(idx5[:, 32 * h : 32 * (h + 1)]))
 
-        def add_rest(i):
-            b, t = tiles[i]
+        def add_rest(c):
+            b, t = ROW_TILES[c]
             if t == 0:
-                rested[b] = slot(rested_tag[b], [P, PACK, 2 * S], BF16, "rested%d" % b)
-            nc.scalar.activation(rested[b][:, t, :], xs[i], ACT.Identity, bias=channel(1, b, t))
+                rested.append(sbuf("rested%d" % b, [P, PACK, 2 * S], BF16, on=("tap_raw01", "line_raw1")[b]))
+            nc.scalar.activation(rested[b][:, t, :], xs[c], ACT.Identity, bias=channel(REST, c))
 
-        def take_abs(ap):
-            nc.scalar.activation(ap, ap, ACT.Abs)
+        def take_abs(slots):
+            nc.scalar.activation(slots, slots, ACT.Abs)
 
-        def interleave(b, h, count):
-            grouped_x[b, h] = slot(("g2", "g3", "h1", "g2")[2 * b + h], [P, S * PACK], BF16, "grouped_x")
+        def interleave(b, h, count, on):
+            x_grouped[b, h] = sbuf("x_grouped%d%d" % (b, h), [P, S * PACK], BF16, on)
             nc.scalar.copy(
-                grouped_x[b, h][:].rearrange("p (c i t) -> p c t i", i=4, t=PACK)[:, :, 0:count, :],
+                x_grouped[b, h][:].rearrange("p (c i t) -> p c t i", i=4, t=PACK)[:, :, 0:count, :],
                 rested[b][:, 0:count, half(h)].rearrange("p t (c i) -> p c t i", i=4),
             )
 
-        def quantise_x(b, h, tag=None):
-            x_q[b, h] = quantise(grouped_x[b, h], "x%d%d" % (b, h), tag)
+        def quantise_x(b, h, on=None):
+            x_q[b, h] = quantise(x_grouped[b, h], "x%d%d" % (b, h), on)
 
-        def deal_read_words(a, tag):
-            dealt = slot(tag, [P, H], I32, "read_words%d" % a)
+        def deal_read_words(a, on):
+            dealt = sbuf("read_words%d" % a, [P, H], I32, on)
             nc.vector.tensor_copy(
-                dealt[:].rearrange("p (b t mo mi) -> p b mo t mi", b=NB, t=PACK, mi=4),
-                read_raw[:, a * H : (a + 1) * H].rearrange("p (b mo mi t) -> p b mo t mi", b=NB, t=PACK, mi=4),
+                dealt[:].rearrange("p (b t mo mi) -> p b mo t mi", b=NB, t=PACK, mi=LINE // 4),
+                read_raw[:, a * H : (a + 1) * H].rearrange("p (b mo mi t) -> p b mo t mi", b=NB, t=PACK, mi=LINE // 4),
             )
             return dealt
 
-        for i in range(2):
-            tap_product(*tiles[i])
+        tap_product(0)
+        tap_product(1)
         put_h2(6)
         put_h2(7)
-        read_plane = deal_plane(read_plane_raw, "read_plane", "w3")
-        make_h1(0, 0)
-        tap_product(*tiles[2])
+        read_plane = deal_plane(read_plane_raw, "read_plane", on="wg2_dealt3")
+        make_sine(0)
+        tap_product(2)
 
-        for i, (b, t) in enumerate(tiles):
-            if i + 1 < len(tiles):
-                make_h1(*tiles[i + 1])
-            put_h1(b, t)
-            fetch(i)
-            if i == 0:
-                tap_q[0, 1] = quantise(tap_grouped[0, 1], "tap01", "page00")
-            if i == 1:
-                tap_q[1, 1] = quantise(tap_grouped[1, 1], "tap11", "page01")
-            if i == 2:
-                read_words = [deal_read_words(0, "page02")]
-            if i + 3 < len(tiles):
-                tap_product(*tiles[i + 3])
-            if i >= 1:
-                add_rest(i - 1)
-                if i < last:
-                    take_abs(xs[i - 1])
-            if i in (PACK, PACK + 1):
-                interleave(0, i - PACK, PACK)
-            if i == PACK:
+        read_words = []
+        for c in range(len(ROW_TILES)):
+            if c < LAST:
+                make_sine(c + 1)
+            put_h1(c)
+            fetch(c)
+            if c < TAP_PASSES:
+                tap_q[c, 1] = quantise(tap_grouped[c, 1], "tap%d1" % c, on="page%d" % c)
+            if c == TAP_PASSES:
+                read_words.append(deal_read_words(0, on="page%d" % c))
+            if c + 3 <= LAST:
+                tap_product(c + 3)
+            if c >= 1:
+                add_rest(c - 1)
+            if 1 <= c < LAST:
+                take_abs(xs[c - 1])
+            if c == PACK:
+                interleave(0, 0, PACK, on="tap_grouped10")
                 quantise_x(0, 0)
+            if c == PACK + 1:
+                interleave(0, 1, PACK, on="tap_grouped00")
 
-        read_words.append(deal_read_words(1, "s1"))
-
-        def finish_x(h):
-            interleave(1, h, PACK - 1)
+        def finish_x(h, on):
+            interleave(1, h, PACK - 1, on)
             nc.scalar.activation(
-                grouped_x[1, h][:].rearrange("p (j t) -> p t j", t=PACK)[:, PACK - 1, :],
-                xs[last][:, half(h)], ACT.Identity, bias=channel(1, *tiles[last]),
+                x_grouped[1, h][:].rearrange("p (j t) -> p t j", t=PACK)[:, PACK - 1, :],
+                xs[LAST][:, half(h)], ACT.Identity, bias=channel(REST, LAST),
             )
-            take_abs(xs[last][:, half(h)])
+            take_abs(xs[LAST][:, half(h)])
 
         out_rows = out.rearrange("(b p t) j -> b t p j", b=NB, t=PACK)
 
         def finish(c, h):
-            b, t = tiles[c]
-            y = bank(("tint", "line", "tap", "turned")[c % 4])
-            for a in range(2):
+            b, t = ROW_TILES[c]
+            y = bank(("tint", "line", "tap", "turned")[t])
+            for a in range(NB):
                 codes, plane = x_q[a, h]
                 nc.tensor.matmul_mx(
                     out=y[:],
-                    lhsT=read_words[a][:, cols(c)].bitcast(FP8X4),
-                    lhsT_scale=read_plane[4 * a : P, cols(c)],
+                    lhsT=read_words[a][:, cols(c)].bitcast(FP8X4), lhsT_scale=read_plane[4 * a : P, cols(c)],
                     rhs=codes[:].bitcast(FP8X4), rhs_scale=plane[:],
-                    start=(a == 0), stop=(a == 1),
+                    start=(a == 0), stop=(a == NB - 1),
                 )
-            res = xs[c][:, half(h)]
-            nc.vector.scalar_tensor_tensor(res, res, channel(2, b, t), y[:], ALU.mult, ALU.add)
-            nc.sync.dma_start(out_rows[b, t][:, h * S : (h + 1) * S], res)
+            result = xs[c][:, half(h)]
+            nc.vector.scalar_tensor_tensor(result, result, channel(LIFT, c), y[:], ALU.mult, ALU.add)
+            nc.sync.dma_start(out_rows[b, t][:, half(h)], result)
 
-        finish_x(0)
+        read_words.append(deal_read_words(1, on="page%d" % LAST))
+        finish_x(0, on="tap_grouped01")
         quantise_x(1, 0)
-        quantise_x(0, 1, "h1")
-        take_abs(xs[last - 1])
-        finish_x(1)
-        for c in range(len(tiles)):
-            if c == last - 1:
+        quantise_x(0, 1, on="x_grouped10")
+        take_abs(xs[LAST - 1])
+        finish_x(1, on="x_grouped00")
+        for c in range(len(ROW_TILES)):
+            if c == LAST - 1:
                 quantise_x(1, 1)
             finish(c, 0)
-        for c in range(len(tiles)):
+        for c in range(len(ROW_TILES)):
             finish(c, 1)

import math
from contextlib import ExitStack

import concourse.mybir as mybir
from concourse.masks import make_identity

F32 = mybir.dt.float32
BF16 = mybir.dt.bfloat16
I32 = mybir.dt.int32
U32 = mybir.dt.uint32
U16 = mybir.dt.uint16
U8 = mybir.dt.uint8
FP8X4 = mybir.dt.float8_e4m3fn_x4
FP4X4 = mybir.dt.float4_e2m1fn_x4
ACT = mybir.ActivationFunctionType
ALU = mybir.AluOpType

P = 128
PACK = 4
BLK = P * PACK
SLOTS = 2048
S = 512
H = 1024
NB = H // BLK
TAP_PASSES = 2
QUADS = 4
LINE = 16
ROW_TILES = [(b, t) for b in range(NB) for t in range(PACK)]
LAST = len(ROW_TILES) - 1
GAIN, REST, LIFT = range(3)
ROUNDER = 12582912.0

FLOPS = 4294967296


def tile_list_slate_cleavage_board_kernel(
    tc, tab_words, tab_scales, tab2_words, tab2_scales, offs, offs2, offs3, offs4, offs5,
    w_tap, gain, w_line, w_tint_words, w_tint_scales, page0, wg1, wg2, rest,
    w_read_words, w_read_scales, lift, out,
):
    nc = tc.nc
    with ExitStack() as ctx:
        lists = ctx.enter_context(tc.tile_pool(name="lists", bufs=1))
        keep = ctx.enter_context(tc.tile_pool(name="keep", bufs=1))
        ring = ctx.enter_context(tc.tile_pool(name="ring", bufs=2))
        psum = ctx.enter_context(tc.psum_pool(name="psum", bufs=2))
        home = {}

        def sbuf(name, shape, dtype, on=None):
            home[name] = home[on] if on else name
            return keep.tile(shape, dtype, name=name, tag=home[name], align_bytes=64)

        def bank(tag):
            return psum.tile([P, S], F32, name=tag, tag=tag)

        def cols(n):
            return slice(n * P, (n + 1) * P)

        def half(h):
            return slice(h * S, (h + 1) * S)

        def load_list(src, name):
            tile = lists.tile(list(src.shape), U16, name=name)
            nc.sync.dma_start(tile[:], src)
            return tile

        def zeroed_plane(engine, name, width):
            plane = sbuf(name, [P, width], U8)
            engine.memset(plane[:].bitcast(I32), 0)
            return plane

        def load_scale_rows(plane, scales):
            rows = 4 * scales.shape[0]
            for q in range(QUADS):
                nc.sync.dma_start(
                    plane[32 * q : 32 * q + rows, :].bitcast(I32),
                    scales[:, 4 * q : 4 * q + 4, :].bitcast(I32),
                )

        def load_table(words, name):
            tile = sbuf(name, [P, SLOTS], U32)
            nc.sync.dma_start(tile[:].bitcast(I32), words.rearrange("p t i -> p (t i)").bitcast(I32))
            return tile

        def load_weight(w, a, b, name):
            raw = sbuf(name, [P, PACK, BLK], F32)
            rows = w[a * BLK : (a + 1) * BLK, b * BLK : (b + 1) * BLK]
            nc.sync.dma_start(raw[:], rows.rearrange("(p j) c -> p j c", j=PACK))
            return raw

        pages = {}

        def load_page(c, on=None):
            b, t = ROW_TILES[c]
            pages[c] = sbuf("page%d" % c, [P, SLOTS], F32, on)
            nc.sync.dma_start(pages[c][:], page0.rearrange("(b p t) s -> b t p s", b=NB, t=PACK)[b, t])

        def load_rows(wg, name, on=None):
            tile = sbuf(name, [P, S], F32, on)
            nc.sync.dma_start(tile[:], wg)
            return tile

        def turn(src, tag):
            turned = bank(tag)
            for jb in range(PACK):
                nc.tensor.transpose(turned[:, cols(jb)], src[:, cols(jb)], ident[:])
            return turned

        def deal_rows(turned, t):
            picked = ring.tile([P, S], F32, name="picked")
            columns = turned[:].rearrange("p (jb m t) -> p jb t m", jb=PACK, t=PACK)[:, :, t, :]
            nc.scalar.copy(
                picked[:].rearrange("p (jb q m) -> p jb q m", jb=PACK, q=QUADS),
                columns.unsqueeze(2).broadcast_to([P, PACK, QUADS, 32]),
            )
            return turn(picked, "turned")

        def gather(window, offsets, dtype, name, on=None):
            picked = sbuf(name, [P, S], dtype, on)
            nc.vector.tensor_copy(picked[:], window[:].indirect(offsets[:]))
            return picked

        def round_weight(copy, raw, name, on=None):
            grouped = sbuf(name, [P, BLK * PACK], BF16, on)
            copy(
                grouped[:].rearrange("p (t m j) -> p m j t", t=PACK, j=PACK),
                raw[:].rearrange("p j (m t) -> p m j t", t=PACK),
            )
            return grouped

        def quantise(grouped, name, on=None):
            codes = sbuf(name + "_codes", [P, BLK], U32, on)
            plane = sbuf(name + "_plane", [P, BLK], U8)
            nc.vector.quantize_mx(out=codes[:].bitcast(FP8X4), scales=plane[:], in_=grouped[:])
            return codes, plane

        def deal_plane(plane, name, on=None):
            dealt = sbuf(name, [P, H], U8, on)
            nc.vector.tensor_copy(
                dealt[:].rearrange("p (b t mo mi) -> p b mo t mi", b=NB, t=PACK, mi=LINE),
                plane[:].rearrange("p (b mo mi t) -> p b mo t mi", b=NB, t=PACK, mi=LINE),
            )
            return dealt

        ident = keep.tile([P, P], F32, name="ident")
        make_identity(nc, ident[:])
        v2_plane_all = zeroed_plane(nc.vector, "v2_plane_all", SLOTS)
        v_plane_all = zeroed_plane(nc.gpsimd, "v_plane_all", SLOTS)
        read_plane_raw = zeroed_plane(nc.gpsimd, "read_plane_raw", H)
        vec_rows = keep.tile([P, BLK], F32, name="vec_rows")
        nc.gpsimd.memset(vec_rows[:], 0.0)

        idx2 = load_list(offs2, "idx2")
        tint_plane_raw = sbuf("tint_plane_raw", [P, H], U8)
        for q in range(QUADS):
            rows = w_tint_scales[0, 4 * q : 4 * q + 4, :].bitcast(I32)
            nc.sync.dma_start(
                tint_plane_raw[32 * q : 32 * q + 32, :].bitcast(I32),
                rows.unsqueeze(0).broadcast_to([8, 4, H // 4]),
            )
        tint_raw = sbuf("tint_raw", [P, 2 * H], U8)
        nc.sync.dma_start(tint_raw[:].bitcast(I32), w_tint_words[0].bitcast(I32))
        wg2_rows = load_rows(wg2, "wg2_rows")
        line_raw = [load_weight(w_line, 0, 0, "line_raw0")]
        load_scale_rows(v2_plane_all, tab2_scales)
        v2_all = load_table(tab2_words[0], "v2_all")
        idx4 = load_list(offs4, "idx4")
        load_scale_rows(v_plane_all, tab_scales)
        idx = load_list(offs, "idx")
        load_page(0)
        wg2_turned = turn(wg2_rows, "tap")
        for v, vec in enumerate((gain, rest, lift)):
            nc.sync.dma_start(vec_rows[NB * v : NB * (v + 1), :], vec.rearrange("(b c) -> b c", b=NB))
        wg1_rows = load_rows(wg1, "wg1_rows", on="wg2_rows")

        tint_words = sbuf("tint_words", [P, 2 * H], U8)
        for b in range(NB):
            run = slice(b * 2 * BLK, (b + 1) * 2 * BLK)
            nc.vector.tensor_copy(
                tint_words[:, run].rearrange("p (t mo mi e) -> p mo t mi e", t=PACK, mi=LINE // 2, e=2),
                tint_raw[:, run].rearrange("p (mo mi t e) -> p mo t mi e", t=PACK, mi=LINE // 2, e=2),
            )
        tint_plane = deal_plane(tint_plane_raw, "tint_plane")
        line_grouped = round_weight(nc.vector.tensor_copy, line_raw[0], "line_grouped0")
        v2_plane = gather(v2_plane_all, idx2, U8, "v2_plane")
        line_q = [quantise(line_grouped, "line0")]
        v2_words = gather(v2_all, idx2, U32, "v2_words")

        load_page(1)
        line_raw.append(load_weight(w_line, 0, 1, "line_raw1"))
        load_page(2)
        v_all = [load_table(tab_words[0], "v_all0")]
        load_page(3)
        v_all.append(load_table(tab_words[1], "v_all1"))
        tap_raw = {}
        for a, b in ((0, 0), (1, 0), (0, 1)):
            tap_raw[a, b] = load_weight(w_tap, a, b, "tap_raw%d%d" % (a, b))
        load_page(4)
        tap_raw[1, 1] = load_weight(w_tap, 1, 1, "tap_raw11")
        load_page(5)
        load_scale_rows(read_plane_raw, w_read_scales)
        idx3 = load_list(offs3, "idx3")
        idx5 = load_list(offs5, "idx5")
        load_page(6)
        load_page(7, on="line_raw0")
        read_raw = sbuf("read_raw", [P, NB * H], I32, on="v2_all")
        nc.sync.dma_start(
            read_raw[:].rearrange("p (a c) -> p a c", a=NB),
            w_read_words.rearrange("a p c i -> p a (c i)").bitcast(I32),
        )

        wg2_dealt, h2 = [], []

        def start_h2(c):
            if c < PACK:
                wg2_dealt.append(sbuf("wg2_dealt%d" % c, [P, S], F32))
                nc.scalar.copy(wg2_dealt[c][:], deal_rows(wg2_turned, c)[:])
            tint = bank("tint")
            nc.tensor.matmul_mx(
                out=tint[:],
                lhsT=tint_words[:, 2 * c * P : 2 * (c + 1) * P].bitcast(FP4X4), lhsT_scale=tint_plane[:, cols(c)],
                rhs=v2_words[:].bitcast(FP8X4), rhs_scale=v2_plane[:], start=True, stop=True,
            )
            h2.append(sbuf("h2_%d" % c, [P, S], F32))
            nc.scalar.copy(h2[c][:], tint[:])

        def put_h2(c):
            b, t = ROW_TILES[c]
            line = bank("line")
            codes, plane = line_q[b]
            nc.tensor.matmul_mx(
                out=line[:],
                lhsT=codes[:, cols(t)].bitcast(FP8X4), lhsT_scale=plane[:, cols(t)],
                rhs=v2_words[:].bitcast(FP8X4), rhs_scale=v2_plane[:], start=True, stop=True,
            )
            nc.vector.tensor_tensor(h2[c][:], line[:], h2[c][:], ALU.min)
            nc.vector.tensor_tensor(pages[c][:].indirect(idx4[:]), h2[c][:], wg2_dealt[t][:], ALU.mult)

        start_h2(0)
        start_h2(1)
        put_h2(0)
        v_plane = gather(v_plane_all, idx, U8, "v_plane")
        put_h2(1)
        for c in range(2, len(ROW_TILES)):
            start_h2(c)
        put_h2(2)
        put_h2(3)
        line_grouped = round_weight(nc.scalar.copy, line_raw[1], "line_grouped1", on="tint_words")
        line_q.append(quantise(line_grouped, "line1", on="h2_3"))
        v_words = [
            gather(v_all[0], idx, U32, "v_words0", on="line_grouped1"),
            gather(v_all[1], idx, U32, "v_words1", on="h2_0"),
        ]
        tap_grouped = {}
        for a, b, on in ((0, 0, "tint_plane"), (1, 0, "line_grouped0"), (0, 1, "h2_1"), (1, 1, "h2_2")):
            tap_grouped[a, b] = round_weight(nc.scalar.copy, tap_raw[a, b], "tap_grouped%d%d" % (a, b), on)

        vec_bank = bank("turned")
        for t in range(PACK):
            nc.tensor.transpose(vec_bank[:, cols(t)], vec_rows[:, t:BLK:PACK], ident[:])
        vec_cols = keep.tile([P, PACK, 3 * NB], F32, name="vec_cols")
        nc.scalar.copy(vec_cols[:], vec_bank[:].rearrange("p (t r) -> p t r", t=PACK)[:, :, 0 : 3 * NB])

        def channel(v, c):
            b, t = ROW_TILES[c]
            return vec_cols[:, t, NB * v + b : NB * v + b + 1]

        put_h2(4)
        tap_q = {
            (0, 0): quantise(tap_grouped[0, 0], "tap00", on="h2_4"),
            (1, 0): quantise(tap_grouped[1, 0], "tap10", on="wg2_dealt0"),
        }
        put_h2(5)

        gated = [keep.tile([P, PACK, S], F32, name="gated%d" % b) for b in range(NB)]
        wg1_turned = turn(wg1_rows, "tint")
        for t in range(PACK):
            dealt = deal_rows(wg1_turned, t)
            for b in range(NB):
                nc.scalar.activation(gated[b][:, t, :], dealt[:], ACT.Copy, scale=channel(GAIN, b * PACK + t))

        fractions, sines = {}, {}

        def tap_product(c):
            b, t = ROW_TILES[c]
            product = bank("tap")
            for jb in range(PACK):
                for a in range(TAP_PASSES):
                    codes, plane = tap_q[a, b]
                    nc.tensor.matmul_mx(
                        out=product[:, cols(jb)],
                        lhsT=v_words[a][:, cols(jb)].bitcast(FP8X4), lhsT_scale=v_plane[4 * a : P, cols(jb)],
                        rhs=codes[:, cols(t)].bitcast(FP8X4), rhs_scale=plane[:, cols(t)],
                        start=(a == 0), stop=(a == TAP_PASSES - 1),
                    )
            turns = ring.tile([P, S], F32, name="turns")
            whole = ring.tile([P, S], U32, name="whole")
            minus_whole = ring.tile([P, S], F32, name="minus_whole")
            nc.scalar.activation(whole[:], product[:], ACT.Copy, scale=0.5 / math.pi, bias=ROUNDER)
            nc.scalar.activation(turns[:], product[:], ACT.Copy, scale=0.5 / math.pi)
            nc.scalar.activation(minus_whole[:], whole[:], ACT.Copy, scale=-1.0, bias=ROUNDER)
            fractions[c] = bank("turned")
            for jb in range(PACK):
                for term, first in ((turns, True), (minus_whole, False)):
                    nc.tensor.matmul(
                        fractions[c][:, cols(jb)], term[:, cols(jb)], ident[:],
                        start=first, stop=not first, is_transpose=True,
                    )

        def make_sine(c):
            sines[c] = sbuf("sine%d" % c, [P, S], F32, on=("h2_7", "read_plane_raw")[c % 2])
            nc.scalar.activation(sines[c][:], fractions[c][:], ACT.Sin, scale=2.0 * math.pi)

        def put_h1(c):
            b, t = ROW_TILES[c]
            nc.vector.tensor_tensor(pages[c][:].indirect(idx3[:]), sines[c][:], gated[b][:, t, :], ALU.mult)

        x_on = ("v_all0", "v_all1", "tap_raw00", "tap_raw11")
        x_pairs, xs, rested, x_grouped, x_q = [], [], [], {}, {}

        def fetch(c):
            if c % 2 == 0:
                x_pairs.append(sbuf("x%d" % c, [P, 2, 2 * S], F32, on=x_on[c // 2]))
            xs.append(x_pairs[c // 2][:, c % 2, :])
            if c < LAST:
                nc.vector.tensor_copy(xs[c], pages[c][:].indirect(idx5[:]))
            else:
                for h in range(2):
                    nc.vector.tensor_copy(xs[c][:, half(h)], pages[c][:].indirect(idx5[:, 32 * h : 32 * (h + 1)]))

        def add_rest(c):
            b, t = ROW_TILES[c]
            if t == 0:
                rested.append(sbuf("rested%d" % b, [P, PACK, 2 * S], BF16, on=("tap_raw01", "line_raw1")[b]))
            nc.scalar.activation(rested[b][:, t, :], xs[c], ACT.Identity, bias=channel(REST, c))

        def take_abs(slots):
            nc.scalar.activation(slots, slots, ACT.Abs)

        def interleave(b, h, count, on):
            x_grouped[b, h] = sbuf("x_grouped%d%d" % (b, h), [P, S * PACK], BF16, on)
            nc.scalar.copy(
                x_grouped[b, h][:].rearrange("p (c i t) -> p c t i", i=4, t=PACK)[:, :, 0:count, :],
                rested[b][:, 0:count, half(h)].rearrange("p t (c i) -> p c t i", i=4),
            )

        def quantise_x(b, h, on=None):
            x_q[b, h] = quantise(x_grouped[b, h], "x%d%d" % (b, h), on)

        def deal_read_words(a, on):
            dealt = sbuf("read_words%d" % a, [P, H], I32, on)
            nc.vector.tensor_copy(
                dealt[:].rearrange("p (b t mo mi) -> p b mo t mi", b=NB, t=PACK, mi=LINE // 4),
                read_raw[:, a * H : (a + 1) * H].rearrange("p (b mo mi t) -> p b mo t mi", b=NB, t=PACK, mi=LINE // 4),
            )
            return dealt

        tap_product(0)
        tap_product(1)
        put_h2(6)
        put_h2(7)
        read_plane = deal_plane(read_plane_raw, "read_plane", on="wg2_dealt3")
        make_sine(0)
        tap_product(2)

        read_words = []
        for c in range(len(ROW_TILES)):
            if c < LAST:
                make_sine(c + 1)
            put_h1(c)
            fetch(c)
            if c < TAP_PASSES:
                tap_q[c, 1] = quantise(tap_grouped[c, 1], "tap%d1" % c, on="page%d" % c)
            if c == TAP_PASSES:
                read_words.append(deal_read_words(0, on="page%d" % c))
            if c + 3 <= LAST:
                tap_product(c + 3)
            if c >= 1:
                add_rest(c - 1)
            if 1 <= c < LAST:
                take_abs(xs[c - 1])
            if c == PACK:
                interleave(0, 0, PACK, on="tap_grouped10")
                quantise_x(0, 0)
            if c == PACK + 1:
                interleave(0, 1, PACK, on="tap_grouped00")

        def finish_x(h, on):
            interleave(1, h, PACK - 1, on)
            nc.scalar.activation(
                x_grouped[1, h][:].rearrange("p (j t) -> p t j", t=PACK)[:, PACK - 1, :],
                xs[LAST][:, half(h)], ACT.Identity, bias=channel(REST, LAST),
            )
            take_abs(xs[LAST][:, half(h)])

        out_rows = out.rearrange("(b p t) j -> b t p j", b=NB, t=PACK)

        def finish(c, h):
            b, t = ROW_TILES[c]
            y = bank(("tint", "line", "tap", "turned")[t])
            for a in range(NB):
                codes, plane = x_q[a, h]
                nc.tensor.matmul_mx(
                    out=y[:],
                    lhsT=read_words[a][:, cols(c)].bitcast(FP8X4), lhsT_scale=read_plane[4 * a : P, cols(c)],
                    rhs=codes[:].bitcast(FP8X4), rhs_scale=plane[:],
                    start=(a == 0), stop=(a == NB - 1),
                )
            result = xs[c][:, half(h)]
            nc.vector.scalar_tensor_tensor(result, result, channel(LIFT, c), y[:], ALU.mult, ALU.add)
            nc.sync.dma_start(out_rows[b, t][:, half(h)], result)

        read_words.append(deal_read_words(1, on="page%d" % LAST))
        finish_x(0, on="tap_grouped01")
        quantise_x(1, 0)
        quantise_x(0, 1, on="x_grouped10")
        take_abs(xs[LAST - 1])
        finish_x(1, on="x_grouped00")
        for c in range(len(ROW_TILES)):
            if c == LAST - 1:
                quantise_x(1, 1)
            finish(c, 0)
        for c in range(len(ROW_TILES)):
            finish(c, 1)
